import numpy as np, ml_dtypes
CORES = [25,29,65,69,153,157,193,197]
N = 8
BF = ml_dtypes.bfloat16
def gentries(a):
    return np.ascontiguousarray(a.reshape(8, 16, -1).transpose(0, 2, 1)).reshape(8, -1)
def gtable(e):
    e = np.asarray(e); return np.ascontiguousarray(e.reshape(8, -1, 16).transpose(0, 2, 1)).reshape(128, -1).astype(np.int32)
V, W, SH, CH, RO = 256, 4096, 2, 3, 3
def parts(rng):
    s = rng.integers(0, 256, (N, 8, 16, W), dtype=np.uint8); x = rng.integers(0, 256, (N, 8, 16, V), dtype=np.uint8)
    r = rng.integers(0, 256, (N, 8, 16, V)); r = np.where(rng.random((N, 8, 1, V)) < 0.5, r, 64 + (r >> 1))
    nx = rng.integers(0, V, (N, 8, V)); sr = rng.integers(0, V, (N, 8, V)); ft = rng.integers(17000, 27000, (N, 8, V))
    return s, r, x, nx, sr, ft
def pack(s, r, x, nx, sr, ft):
    return {"prof": s.reshape(N, 128, W).astype(np.float32).astype(BF), "resid": np.ascontiguousarray(r.reshape(N, 128, V)).astype(np.int32), "obs": x.reshape(N, 128, V).astype(np.float32).astype(BF),
            "nx0": np.stack([gtable(a) for a in nx]), "src0": np.stack([gtable(a) for a in sr]), "fit0": np.ascontiguousarray(ft.reshape(N, 8, V)).astype(np.int32)}
def setup_inputs(rng):
    return pack(*parts(rng))
def setup_inputs_spread(rng):
    s = np.minimum(np.exp2(8 * rng.random((N, 8, 1, W))) * rng.random((N, 8, 16, W), dtype=np.float32), 255).astype(np.uint8)
    x = np.minimum(np.exp2(8 * rng.random((N, 8, 1, V))) * rng.random((N, 8, 16, V)), 255).astype(np.uint8)
    r = np.minimum(np.exp2(8 * rng.random((1, 8, 16, 1))) * rng.random((N, 8, 16, V)), 255).astype(np.int64)
    nx = np.minimum((V * rng.random((N, 8, V)) ** 3).astype(np.int64), V - 1); sr = V - 1 - np.minimum((V * rng.random((N, 8, V)) ** 3).astype(np.int64), V - 1)
    ft = np.minimum(np.exp2(16 * rng.random((N, 8, V)) ** 0.5), 65535).astype(np.int64)
    return pack(s, r, x, nx, sr, ft)
def setup_inputs_ends(rng):
    s, r, x, nx, sr, ft = parts(rng)
    s = 255 * rng.integers(0, 2, (N, 8, 16, W), dtype=np.uint8); x = 255 * rng.integers(0, 2, (N, 8, 16, V), dtype=np.uint8)
    cnt = np.clip(np.array([8, 16, 8, 0, 8, 16, 8, 8])[None, :, None] + rng.integers(-1, 2, (N, 8, V)), 0, 16)
    r = np.where(np.argsort(rng.random((N, 8, 16, V)), axis=2) < cnt[:, :, None, :], 255, 0)
    alt = 255 * (np.arange(16) & 1); r[:, 7, :, 0] = alt; r[:, 7, :, V - 1] = 255 - alt; r[N - 1, 7, 15, V - 1] = 255
    for q in range(N):
        for g in range(8):
            if (N - 1 - q + 7 - g) % 2 == 0:
                bit = rng.permutation(np.array([0, 1] + [int(b) for b in rng.integers(0, 2, 14)])).astype(np.uint8); row = (255 * bit)[:, None]
                s[q, g] = row; kind = rng.integers(0, 4, V); kind[0] = 0; kind[V - 1] = 0
                x[q, g] = np.where(kind[None, :] < 2, 255 - row, np.where(kind[None, :] == 2, row, x[q, g]))
    ft = np.where(rng.random((N, 8, V)) < 0.7, 65535, 0); ft[:, :, 0] = 65535; ft[:, :, V - 1] = 65535
    nx = np.where(rng.random((N, 8, V)) < 0.8, (V - 1) * rng.integers(0, 2, (N, 8, V)), nx); sr = np.where(rng.random((N, 8, V)) < 0.8, (V - 1) * rng.integers(0, 2, (N, 8, V)), sr)
    nx[:, :, V - 1] = V - 1; sr[:, :, V - 1] = 0
    return pack(s, r, x, nx, sr, ft)
def setup_inputs_corners(rng):
    s, r, x, nx, sr, ft = parts(rng); own = np.arange(V)
    for q in range(N):
        r[q, 0:2] = rng.integers(0, 8, (2, 16, V)) if q % 2 == 0 else rng.integers(248, 256, (2, 16, V))
    v = rng.integers(0, 2, (N, 2, 8, V)); e = 128 + np.concatenate([v, -v], axis=2)
    e = np.take_along_axis(e, np.argsort(rng.random(e.shape), axis=2), 2)
    d = np.where((own & 1) == 1, rng.choice(np.array([-129, -128, -127, -1, 0, 1, 126, 127, 128]), (N, 2, V)), 0)
    e[:, :, 0] += d >> 1; e[:, :, 15] += d - (d >> 1); r[:, 2:4] = e
    nx[:, 2:4] = 2 * rng.integers(0, V // 2, (N, 2, V)); sr[:, 2:4] = 2 * rng.integers(0, V // 2, (N, 2, V))
    top = rng.random((N, 1, V)) < 0.5; low = np.zeros((N, 16, V), np.int64)
    np.put_along_axis(low, rng.integers(0, 16, (N, 1, V)), rng.choice(np.array([0, 0, 1, 2, 100, 254, 255]), (N, 1, V)), 1)
    r[:, 4] = np.where(top, 255 - low, low)
    for q in range(N):
        for g in range(8):
            m = (q + g) % 6
            if g not in (2, 3):
                if m == 0: nx[q, g] = own; sr[q, g] = own
                if m == 1: nx[q, g] = 0; sr[q, g] = V - 1
                if m == 2: nx[q, g] = V - 1; sr[q, g] = 0
                if m == 3: nx[q, g] = own; sr[q, g] = (own + 1) % V
                if m == 4: nx[q, g] = np.stack([0 * own, 0 * own + V - 1, own])[rng.integers(0, 3, V), own]
            m = (2 * q + g) % 5
            if m == 0: ft[q, g] = 0
            if m == 1: ft[q, g] = 65535
            if m == 2: ft[q, g] = rng.choice(np.array([0, 1, 7, 8, 20000, 65279, 65280, 65281, 65535]), V)
    return pack(s, r, x, nx, sr, ft)
def setup_inputs_near(rng):
    s, r, x, nx, sr, ft = parts(rng); own = np.arange(V)
    mid = 112 + (r[:, 5:7] & 15); s = s & 3; x = x & 3; r[:, ::2] = r[:, ::2] & 3; r[:, 5:7] = mid
    sr = np.where(rng.random((N, 8, V)) < 0.25, own, sr); ft = rng.integers(285, 336, (N, 8, V))
    ft[:, 5:7] = np.where(rng.random((N, 2, V)) < 0.5, 65535, ft[:, 5:7])
    return pack(s, r, x, nx, sr, ft)
def setup_inputs_rounds(rng):
    s, r, x, nx, sr, ft = parts(rng); m = V - N; e = np.arange(m); st = (3 * e) // m
    for g in range(8):
        if g in (3, 7):
            s[:, g] = s[:, g] & 3; x[:, g] = x[:, g] & 3; r[:, g] = 112 + (r[:, g] & 7); ft[:, g] = 65535
            continue
        o = rng.permutation(V); tg = o[:N]
        for q in range(N):
            row = 255 * rng.integers(0, 2, (16, 1)); kind = rng.integers(0, 3, (1, V))
            d = np.where(kind == 0, 255, np.where(kind == 1, 255 - rng.integers(0, 101, (16, V)), rng.integers(0, 128, (16, V))))
            s[q, g] = row.astype(np.uint8); x[q, g] = np.where(row == 0, d, 255 - d).astype(np.uint8)
            mid = 112 + (r[q, g] & 7); mid[:, tg[np.arange(N) != q]] = rng.integers(0, 8, (16, N - 1)) + 248 * rng.integers(0, 2, (1, N - 1)); r[q, g] = mid
            sl = rng.permutation(o[N:]); nx[q, g, tg] = tg; sr[q, g, tg] = tg; nx[q, g, sl] = tg[(q + 1 + st) % N]
            w = 1 + (q + 3 * g) % 7; c = 8 * int(rng.integers(1, 4)) + w
            later = e % (w + 1) if (q + g) % 2 == 0 else e % 10
            off = np.where(st == 0, np.where(e < c, 1 + e % 9, -(e % 9)), np.where(st == 1, later, e % 10))
            ft[q, g] = 0; ft[q, g, sl] = np.maximum(16 * np.add.reduce(d, axis=0)[sl] + off, 0)
    return pack(s, r, x, nx, sr, ft)
def check_inputs(d):
    bad = []
    for k, lo, hi in (("prof", 0, 255), ("resid", 0, 255), ("obs", 0, 255), ("nx0", 0, V - 1), ("src0", 0, V - 1), ("fit0", 0, 65535)):
        v = np.asarray(d[k]).astype(np.float64)
        if not (np.min(v) >= lo and np.max(v) <= hi): bad.append("range of " + k)
        elif np.any(v != np.floor(v)): bad.append("whole numbers of " + k)
    return bad
def reference(prof, resid, obs, nx0, src0, fit0):
    sp = np.ascontiguousarray(prof.astype(np.float32).astype(np.int16).reshape(N, 8, 16, W).transpose(0, 1, 3, 2)).reshape(N, 8 * W, 16)
    ob = np.ascontiguousarray(obs.astype(np.float32).astype(np.int16).reshape(N, 8, 16, V).transpose(0, 1, 3, 2))
    r = resid.astype(np.int64).reshape(N, 8, 16, V); ft = fit0.astype(np.int64)
    nx = np.stack([gentries(a) for a in nx0]).astype(np.int64); sr = np.stack([gentries(a) for a in src0]).astype(np.int64)
    acc = np.zeros((N, 8), np.int64); odd = 2 * np.arange(V) + 1; first = (np.arange(8) * W)[:, None, None]; site = np.arange(16)[None, :, None]; none = 2 ** 20
    def cost(a, p):
        col = ((odd * (p + 4096)) >> SH) & (W - 1)
        return np.add.reduce(np.abs(np.take(sp[a], first + col, axis=0) - ob[a][:, None]), axis=-1, dtype=np.int64)
    for t in range(RO):
        tot = np.add.reduce(r, axis=2); r2, nx2, sr2, ft2, took = [], [], [], [], []
        for a in range(N):
            q = (a + 1 + t % (N - 1)) % N; n = nx[a]
            best = np.full((8, V), none, np.int64); bn = np.zeros((8, V), np.int64); bl = r[a]
            for z in range(CH):
                if z > 0: n = np.take_along_axis(sr[q], n, 1)
                l = np.take_along_axis(r[q], n[:, None, :], 2)
                dl = (tot[a] - np.take_along_axis(tot[q], n, 1))[:, None, :]
                p = np.add.accumulate(l, axis=1); g = cost(a, p); h = cost(a, p + dl)
                sc = np.add.accumulate(g, axis=1) - g + np.add.accumulate(h[:, ::-1], axis=1)[:, ::-1]
                sc = np.where((l + dl >= 0) & (l + dl <= 255), sc, none)
                j = np.argmin(sc, axis=1); m = np.min(sc, axis=1); better = m < best
                bl = np.where(better[:, None, :], l + np.where(site == j[:, None, :], dl, 0), bl)
                bn = np.where(better, n, bn); best = np.where(better, m, best)
            ok = best < ft[a] - (acc[a] & 7)[:, None]
            r2.append(np.where(ok[:, None, :], bl, r[a])); ft2.append(np.where(ok, best, ft[a])); sr2.append(np.where(ok, bn, sr[a]))
            nx2.append(np.where(ok, (13 * bn + best) & (V - 1), n)); took.append(np.add.reduce(ok.astype(np.int64), axis=1))
        r, nx, sr, ft = np.stack(r2), np.stack(nx2), np.stack(sr2), np.stack(ft2); acc = acc + np.stack(took)
    return {"yr": r.reshape(N, 128, V).astype(np.float32), "yf": ft.astype(np.float32), "yn": nx.astype(np.float32)}

@@ -1,0 +1,537 @@
+import numpy as np
+from concourse.bass import DstId, RemoteDMATransfer
+from concourse.mybir import dt, AluOpType, AxisListType, ActivationFunctionType
+
+AL = AluOpType
+AF = ActivationFunctionType
+NR = 3
+V = 256
+SA = 144
+ABLK = [(0, 32), (32, 64), (64, 96), (96, 128), (128, 144)]
+DBLK = [(144, 176), (176, 208), (208, 240), (240, 256)]
+CHUNKS = [[("A", 0, 32)], [("A", 32, 96)], [("A", 96, 144)],
+          [("D", 144, 176), ("D", 176, 208)], [("D", 208, 240), ("D", 240, 256)]]
+ORDER = ["A0", "D0", "A1", "D1", "A2", "D2", "A3", "D3", "A4"]
+KEYBANK = [(0, 96, "psKA"), (96, 144, "psKB"), (144, 256, "psKC")]
+PAY = 288
+BIG = 33554432.0
+MAGIC = 1.5 * 2.0 ** 31
+
+SCRATCH = {
+    "S": ("sbuf", [128, 4096], "bfloat16"), "obs_s": ("sbuf", [128, 256], "bfloat16"), "nobs": ("sbuf", [128, 256], "float32"),
+    "Xe": ("sbuf", [128, (V - SA) * 48], "bfloat16"),
+    "rawR": ("sbuf", [128, 256], "int32"), "raws": ("sbuf", [128, 16], "int32"), "rawn": ("sbuf", [128, 16], "int32"),
+    "fitb": ("sbuf", [128, 256], "int32"), "fitf": ("sbuf", [128, 256], "float32"), "fitt": ("sbuf", [128, 256], "float32"),
+    "W0": ("sbuf", [128, 1056], "bfloat16"), "W1": ("sbuf", [128, 1056], "bfloat16"), "W2": ("sbuf", [128, 1056], "bfloat16"),
+    "land0": ("sbuf", [128, PAY], "bfloat16"), "land1": ("sbuf", [128, PAY], "bfloat16"), "land2": ("sbuf", [128, PAY], "bfloat16"),
+    "LQ1": ("sbuf", [128, 256], "bfloat16"), "LQ2": ("sbuf", [128, 256], "bfloat16"),
+    "srcU": ("sbuf", [128, 16], "uint16"), "n0U": ("sbuf", [128, 16], "uint16"), "offB": ("sbuf", [128, 32], "uint16"),
+    "B1": ("sbuf", [128, 256], "bfloat16"), "X": ("sbuf", [128, 256], "bfloat16"), "X2": ("sbuf", [128, 256], "bfloat16"),
+    "nX": ("sbuf", [128, 512], "bfloat16"), "T12": ("sbuf", [128, 512], "bfloat16"),
+    "off": ("sbuf", [128, 1536], "uint16"), "odd": ("sbuf", [128, 1536], "float32"),
+    "v1a": ("sbuf", [128, 384], "int32"), "v1b": ("sbuf", [128, 384], "int32"), "v2a": ("sbuf", [128, 384], "int32"), "v2b": ("sbuf", [128, 384], "int32"),
+    "pen": ("sbuf", [128, 768], "bfloat16"),
+    "A": ("sbuf", [128, SA * 96], "bfloat16"), "dd": ("sbuf", [128, (V - SA) * 96], "bfloat16"), "rr": ("sbuf", [128, (V - SA) * 96], "bfloat16"),
+    "z1": ("sbuf", [128, 768], "float32"), "tr": ("sbuf", [128, 256], "float32"), "s2": ("sbuf", [128, 256], "int32"),
+    "sc": ("sbuf", [128, 16], "int32"), "z16": ("sbuf", [128, 16], "int32"), "st": ("sbuf", [128, 16], "int32"),
+    "acc0": ("sbuf", [128, 32], "bfloat16"), "acc1": ("sbuf", [128, 32], "bfloat16"), "acc2": ("sbuf", [128, 32], "bfloat16"),
+    "SWa": ("sbuf", [128, 32], "bfloat16"), "nL": ("sbuf", [128, 16], "bfloat16"), "nLn": ("sbuf", [128, 16], "bfloat16"), "srcb": ("sbuf", [128, 16], "bfloat16"),
+    "F": ("sbuf", [128, 16], "float32"), "thr": ("sbuf", [128, 16], "float32"), "Ai": ("sbuf", [128, 16], "int32"), "A7": ("sbuf", [128, 16], "int32"),
+    "dn1": ("sbuf", [128, 16], "float32"), "dn2": ("sbuf", [128, 16], "float32"),
+    "e2": ("sbuf", [128, 16], "float32"), "e3": ("sbuf", [128, 16], "float32"), "t2": ("sbuf", [128, 16], "float32"), "t3": ("sbuf", [128, 16], "float32"),
+    "b1": ("sbuf", [128, 16], "float32"), "bn": ("sbuf", [128, 16], "float32"), "d1": ("sbuf", [128, 16], "float32"), "d2": ("sbuf", [128, 16], "float32"),
+    "h1": ("sbuf", [128, 16], "float32"), "h2": ("sbuf", [128, 16], "int32"), "h3": ("sbuf", [128, 16], "int32"), "d3": ("sbuf", [128, 16], "float32"), "d4": ("sbuf", [128, 16], "float32"),
+    "d5": ("sbuf", [128, 16], "float32"), "d6": ("sbuf", [128, 16], "float32"),
+    "Rb": ("sbuf", [128, 256], "bfloat16"), "OH": ("sbuf", [128, 256], "bfloat16"), "md": ("sbuf", [128, 256], "bfloat16"),
+    "Rf": ("sbuf", [128, 256], "float32"), "B2": ("sbuf", [128, 256], "float32"), "oT": ("sbuf", [128, 256], "float32"),
+    "ones": ("sbuf", [128, 128], "bfloat16"), "I": ("sbuf", [128, 128], "bfloat16"), "BLK": ("sbuf", [128, 128], "bfloat16"), "TRI": ("sbuf", [128, 128], "bfloat16"),
+    "TMO": ("sbuf", [128, 128], "bfloat16"), "IMO": ("sbuf", [128, 128], "bfloat16"), "NBLK": ("sbuf", [128, 128], "bfloat16"), "BIGI": ("sbuf", [128, 128], "bfloat16"),
+    "BLK32": ("sbuf", [128, 128], "bfloat16"), "B48": ("sbuf", [128, 8, 48], "bfloat16"), "WT": ("sbuf", [128, 248, 16], "bfloat16"),
+    "E": ("sbuf", [128, 512], "bfloat16"), "E16": ("sbuf", [128, 512], "bfloat16"),
+    "c4096": ("sbuf", [128, 64], "bfloat16"), "cm127": ("sbuf", [128, 64], "bfloat16"),
+    "pi": ("sbuf", [128, 1], "int32"), "pj": ("sbuf", [128, 1], "int32"), "jcol": ("sbuf", [128, 1], "float32"),
+    "kct": ("sbuf", [128, 96], "float32"), "KC": ("sbuf", [128, 96], "bfloat16"),
+    "ilt": ("sbuf", [128, 16], "float32"), "ilist": ("sbuf", [128, 16], "bfloat16"), "zit": ("sbuf", [128, 16], "float32"), "ZI": ("sbuf", [128, 16], "bfloat16"),
+    "RS3": ("sbuf", [128, 336], "float32"), "RS16": ("sbuf", [128, 256], "float32"),
+    "psP0": ("psum", [128, 512], "float32"), "psP1": ("psum", [128, 512], "float32"), "psQ": ("psum", [128, 512], "float32"),
+    "psKA": ("psum", [128, 512], "float32"), "psKB": ("psum", [128, 512], "float32"), "psKC": ("psum", [128, 512], "float32"),
+    "psS": ("psum", [128, 512], "float32"), "psD": ("psum", [128, 512], "float32"),
+}
+SEMAPHORES = (["qv", "qa", "qp", "qg"] + ["ld%d" % i for i in range(6)] + ["st%d" % i for i in range(3)]
+              + ["%s%d" % (n, t) for n in ("arr", "hop", "loc", "hl") for t in range(NR)])
+
+
+def route(q, t, cores, topo):
+    n = len(cores)
+    src, dst = cores[q], cores[(q - 1 - (t % (n - 1))) % n]
+    if topo.may_write(src, dst):
+        return dst, None
+    for c in topo.cores_of(src):
+        if c not in cores and topo.die(c) == topo.die(src) and topo.may_write(c, dst):
+            return dst, c
+    return dst, None
+
+
+def pick(src, dst, topo):
+    e = topo.engines(src, dst)[:8]
+    return sum(1 << i for i in e), len(e)
+
+
+def relay_program(g, core, T, topo):
+    for t in range(NR):
+        for q in range(len(T.cores)):
+            dst, via = route(q, t, T.cores, topo)
+            if via != core:
+                continue
+            _, n1 = pick(T.cores[q], core, topo)
+            m, n2 = pick(core, dst, topo)
+            rid, pid = topo.addr(dst, core)
+            land = T["land%d" % t]
+            g.wait_ge(T.sem["hop%d" % t], n1)
+            g.remote_dma(out_ap=land[:], in_ap=land[:], remote_sem=T.sem["arr%d" % t], local_sem=T.sem["hl%d" % t],
+                         pid=pid, routing_id=rid, dma_engine_mask=m)
+    for t in range(NR):
+        for q in range(len(T.cores)):
+            dst, via = route(q, t, T.cores, topo)
+            if via == core:
+                g.wait_ge(T.sem["hl%d" % t], pick(core, dst, topo)[1])
+
+
+def rank_program(g, core, T, topo):
+    rank = T.rank_of(core)
+    if rank is None:
+        relay_program(g, core, T, topo)
+        return
+    ENG = {"v": g.vector, "a": g.scalar, "p": g.tensor, "g": g, "s": g.sync}
+    total, known, hist, rec, bank = {}, {k: {} for k in ENG}, {}, {}, {}
+    nload = [0]
+
+    def need(want, tok):
+        s, c = tok
+        if want.get(s, 0) < c:
+            want[s] = c
+
+    def learn(q, s, c):
+        k = known[q]
+        for a, b in hist.get((s, c), {}).items():
+            if k.get(a, 0) < b:
+                k[a] = b
+        if k.get(s, 0) < c:
+            k[s] = c
+
+    def wait(q, want):
+        for s, c in sorted(want.items(), key=lambda x: x[0]):
+            if known[q].get(s, 0) < c:
+                ENG[q].wait_ge(T.sem[s], c)
+                learn(q, s, c)
+
+    def step(v):
+        return v[4] if len(v) > 4 else 1
+
+    def clash(r, v):
+        s = step(v)
+        return r[1] < v[3] and v[2] < r[2] and not (s > 1 and s == r[5] and (r[1] - v[2]) % s)
+
+    def covers(v, r):
+        s = step(v)
+        return v[2] <= r[1] and r[2] <= v[3] and (s == 1 or (s == r[5] and (r[1] - v[2]) % s == 0))
+
+    def op(q, fn, reads, writes, sem=None, inc=1, then=True):
+        own = sem is None
+        s = "q" + q if own else sem
+        tag = q if own else "x" + sem
+        want = {}
+        for v in reads:
+            if v[1][:2] == "ps":
+                for a, tok in bank.get(v[1], {}).items():
+                    if a != tag:
+                        need(want, tok)
+                continue
+            for r in rec.get(v[1], []):
+                if r[0] == "w" and clash(r, v):
+                    need(want, r[4])
+        for v in writes:
+            if v[1][:2] == "ps":
+                for a, tok in bank.get(v[1], {}).items():
+                    if a != tag:
+                        need(want, tok)
+                continue
+            for r in rec.get(v[1], []):
+                if (r[3] != tag or r[0] == "w") and clash(r, v):
+                    need(want, r[4])
+        wait(q, want)
+        ins = fn(ENG[q])
+        total[s] = total.get(s, 0) + inc
+        tok = (s, total[s])
+        if then:
+            ins.then_inc(T.sem[s], inc)
+        hist[tok] = dict(known[q])
+        for v in reads:
+            if v[1][:2] == "ps":
+                bank.setdefault(v[1], {})[tag] = tok
+                continue
+            L = [r for r in rec.get(v[1], []) if not (r[0] == "r" and r[3] == tag and covers(v, r))]
+            L.append(("r", v[2], v[3], tag, tok, step(v)))
+            rec[v[1]] = L
+        for v in writes:
+            if v[1][:2] == "ps":
+                bank.setdefault(v[1], {})[tag] = tok
+                continue
+            L = [r for r in rec.get(v[1], []) if not covers(v, r)]
+            L.append(("w", v[2], v[3], tag, tok, step(v)))
+            rec[v[1]] = L
+        return tok
+
+    def arrived(name, lo, hi, sem, n):
+        total[sem] = total.get(sem, 0) + n
+        rec.setdefault(name, []).append(("w", lo, hi, "x" + sem, (sem, total[sem]), 1))
+
+    def B(name, lo=0, hi=None, step=1):
+        t = T[name]
+        hi = t.shape[1] if hi is None else hi
+        return (t[:, lo:hi] if step == 1 else t[:, lo:hi:step], name, lo, hi, step)
+
+    def ind(win, of):
+        return win[0].indirect(of[0])
+
+    def tt(out, a, b, o):
+        return op("v", lambda e: e.tensor_tensor(out[0], a[0], b[0], o), [a, b], [out])
+
+    def ts(out, a, s1, s2, o0, o1=None, col=None):
+        x = col[0] if col else s1
+        if o1 is None:
+            return op("v", lambda e: e.tensor_scalar(out[0], a[0], x, None, o0), [a] + ([col] if col else []), [out])
+        return op("v", lambda e: e.tensor_scalar(out[0], a[0], x, s2, o0, o1), [a] + ([col] if col else []), [out])
+
+    def vcopy(out, a):
+        return op("v", lambda e: e.tensor_copy(out[0], a[0]), [a], [out])
+
+    def vgather(out, win, of):
+        return op("v", lambda e: e.tensor_copy(out[0], ind(win, of)), [win, of], [out])
+
+    def agather(out, win, of):
+        return op("a", lambda e: e.activation(out[0], ind(win, of), AF.Copy), [win, of], [out])
+
+    def vtrans(out, a):
+        return op("v", lambda e: e.transpose(out[0], a[0]), [a], [out])
+
+    def memset(out, c):
+        return op("v", lambda e: e.memset(out[0], c), [], [out])
+
+    def scan(out, d0, d1):
+        return op("v", lambda e: e.tensor_tensor_scan(out[0], d0[0], d1[0], 0.0, AL.add, AL.min), [d0, d1], [out])
+
+    def mm(out, l, r, start, stop):
+        return op("p", lambda e: e.matmul(out[0], l[0], r[0], start, stop), [l, r], [out])
+
+    def load(q, out, src):
+        k = nload[0]
+        nload[0] += 1
+        return op(q, lambda e: e.dma_start(out[0], src), [], [out], sem="ld%d" % k, inc=16)
+
+    def iota(out, pattern, base, cm, f=True):
+        if f:
+            return op("g", lambda e: e.iota(out[0], pattern, base, cm, allow_small_or_imprecise_dtypes=True), [], [out])
+        return op("g", lambda e: e.iota(out[0], pattern, base, cm), [], [out])
+
+    def sel(out, a, pattern, cmp, base, cm):
+        return op("g", lambda e: e.affine_select(out[0], a[0], pattern, cmp, 0.0, base, cm), [a], [out])
+
+    def weight(gh, k):
+        n = 15 * gh + k
+        return (T.WT[:, 8 * n:8 * n + 8, :], "WT", n, n + 1)
+
+    def put_weight(gh, k, q):
+        lo = 15 - k if gh == 0 else 31 - k
+        i, o = (T.B48[:, :, lo:lo + 16], "B48", 0, 384), weight(gh, k)
+        if q == "v":
+            return vcopy(o, i)
+        return op("a", lambda e: e.activation(o[0], i[0], AF.Copy), [i], [o])
+
+    def swap(field, col, extra=None, name="E"):
+        fb, fo = field
+        for h in range(2):
+            o = B("psS", col + h, col + 16, 2)
+            if extra is not None:
+                mm(o, B("I"), B(extra, h, 16, 2), True, False)
+            for e in range(2):
+                k = 128 * (2 * e + h)
+                mm(o, B(name, k, k + 128), B(fb, fo + e, fo + 16, 2), extra is None and e == 0, e == 1)
+
+    W = ["W0", "W1", "W2"]
+    load("s", B("rawR"), T.resid[:])
+    load("a", B("raws"), T.src0[:])
+    load("a", B("rawn"), T.nx0[:])
+    load("s", B("S"), T.prof[:])
+    load("a", B("obs_s"), T.obs[:])
+    memset(B("ones"), 1.0)
+    memset(B("E"), 0.0)
+    memset(B("fitb"), 0)
+    op("v", lambda e: e.memset(T.B48[:, :, 0:16], 0.0), [], [("", "B48", 0, 384)])
+    op("v", lambda e: e.memset(T.B48[:, :, 16:32], 64.0), [], [("", "B48", 0, 384)])
+    op("v", lambda e: e.memset(T.B48[:, :, 32:48], 0.0), [], [("", "B48", 0, 384)])
+    op("a", lambda e: e.dma_start(T.fitb[0:128:16, :], T.fit0[:]), [], [B("fitb")], sem="ld5", inc=16)
+    iota(B("pi"), [[0, 1]], 0, 1, False)
+    sel(B("I"), B("ones"), [[-1, 128]], AL.is_equal, 0, 1)
+    iota(B("ilt"), [[16, 16]], 0, 0)
+    iota(B("zit"), [[1, 16]], 0, 0)
+    iota(B("kct"), [[0, 32], [16, 3]], 16, 0)
+    for e in range(2):
+        for h in range(2):
+            for a in range(4):
+                k = 128 * (2 * e + h) + 32 * a
+                vcopy(B("E", k + 16 * e, k + 16 * e + 16), B("I", 32 * a + 16 * h, 32 * a + 16 * h + 16))
+    ts(B("E16"), B("E"), 16.0, None, AL.mult)
+    vcopy(B("W0", 0, 16), B("raws"))
+    swap(("W0", 0), 0)
+    vcopy(B("W0", 16, 32), B("psS", 0, 16))
+    vcopy(B("W0", 32, 288), B("rawR"))
+    sel(B("BLK"), B("ones"), [[-16, 8], [0, 16]], AL.is_ge, 0, 1)
+    sel(B("BLK"), B("BLK"), [[16, 8], [0, 16]], AL.is_ge, 15, -1)
+    sel(B("TRI"), B("BLK"), [[1, 128]], AL.is_ge, 0, -1)
+
+    def send(t):
+        dst, via = route(rank, t, T.cores, topo)
+        to = dst if via is None else via
+        m, n = pick(core, to, topo)
+        rid, pid = topo.addr(to, core)
+        rs = T.sem[("arr%d" if via is None else "hop%d") % t]
+        src = B(W[t], 0, PAY)
+        op("g", lambda e: e.remote_dma(out_ap=T["land%d" % t][:], in_ap=src[0], remote_sem=rs, local_sem=T.sem["loc%d" % t],
+                                       pid=pid, routing_id=rid, dma_engine_mask=m), [src], [], sem="loc%d" % t, inc=n, then=False)
+
+    def expect(t):
+        for q in range(len(T.cores)):
+            dst, via = route(q, t, T.cores, topo)
+            if dst == core:
+                arrived("land%d" % t, 0, PAY, "arr%d" % t, pick(T.cores[q] if via is None else via, core, topo)[1])
+
+    send(0)
+    b48 = (T.B48[:], "B48", 0, 384)
+    sel(b48, b48, [[-16, 8], [0, 48]], AL.is_ge, 0, 1)
+    sel(b48, b48, [[16, 8], [0, 48]], AL.is_ge, 15, -1)
+    iota(B("odd", 0, 6 * SA), [[2, SA], [0, 6]], 1, 0)
+    for s0, s1 in DBLK:
+        iota(B("odd", 6 * s0, 6 * s1), [[0, 2], [2, s1 - s0], [0, 3]], 2 * s0 + 1, 0)
+    sel(B("BLK32"), B("ones"), [[-32, 4], [0, 32]], AL.is_ge, 0, 1)
+    sel(B("BLK32"), B("BLK32"), [[32, 4], [0, 32]], AL.is_ge, 31, -1)
+    vcopy(B("nL"), B("rawn"))
+    swap(("nL", 0), 32)
+    vcopy(B("n0U"), B("rawn"))
+    vcopy(B("nLn"), B("psS", 32, 48))
+    ts(B("pj"), B("pi"), 15, None, AL.bitwise_and)
+    vcopy(B("jcol"), B("pj"))
+    ts(B("KC"), B("kct"), None, None, AL.add, col=B("jcol"))
+    ts(B("ilist"), B("ilt"), None, None, AL.add, col=B("jcol"))
+    ts(B("ZI"), B("zit"), None, None, AL.is_equal, col=B("jcol"))
+    memset(B("c4096"), 4096.0)
+    memset(B("cm127"), -127.5)
+    tt(B("TMO"), B("TRI"), B("BLK"), AL.subtract)
+    tt(B("IMO"), B("I"), B("BLK"), AL.subtract)
+    ts(B("NBLK"), B("BLK"), -1.0, None, AL.mult)
+    ts(B("BIGI"), B("I"), 4194304.0, None, AL.mult)
+    memset(B("B1"), 0.0)
+    memset(B("RS3"), 0.0)
+    memset(B("RS3", 0, 336, 3), BIG)
+    memset(B("RS16"), 0.0)
+    memset(B("RS16", 0, 256, 16), BIG)
+    ts(B("nobs"), B("obs_s"), -1.0, None, AL.mult)
+    for k in range(48):
+        o, i = B("Xe", k, (V - SA) * 48, 48), B("obs_s", SA, V)
+        if k % 2:
+            op("a", lambda e: e.activation(o[0], i[0], AF.Copy), [i], [o])
+        else:
+            vcopy(o, i)
+    for gh in range(2):
+        for k in range(15 + gh):
+            put_weight(gh, k, "a" if k % 2 else "v")
+    vcopy(B("fitf"), B("fitb"))
+    vtrans(B("fitt"), B("fitf"))
+    vcopy(B("F"), B("fitt", 0, 256, 16))
+    vcopy(B("thr"), B("F"))
+
+    nown = ["nLn"]
+    for t in range(NR):
+        w, land = W[t], "land%d" % t
+        expect(t)
+
+        def ro(a, b, w=w):
+            return B(w, 32 + a, 32 + b)
+
+        def rc(z, a, b, w=w):
+            return B(w, 32 + 256 * (z + 1) + a, 32 + 256 * (z + 1) + b)
+        lists = B(land, 32, 288)
+        vcopy(B("srcU"), B(land, 0, 16))
+        agather(B("LQ1"), lists, B("srcU"))
+        vgather(rc(0, 0, 256), lists, B("n0U"))
+        agather(B("LQ2"), B("LQ1"), B("srcU"))
+        vgather(rc(1, 0, 256), B("LQ1"), B("n0U"))
+        vgather(rc(2, 0, 256), B("LQ2"), B("n0U"))
+        vcopy(B("B1", 0, 256, 16), B(land, 16, 32))
+        vtrans(B("X"), B("B1"))
+        agather(B("X2"), B("X"), B("srcU"))
+        agather(B("nX", 0, 256), B("X"), B("n0U"))
+        agather(B("nX", 256, 512), B("X2"), B("n0U"))
+        for ci, ch in enumerate(CHUNKS):
+            c0, c1 = ch[0][1], ch[-1][2]
+            P = "psP%d" % (ci % 2)
+            for kind, s0, s1 in ch:
+                n = s1 - s0
+                for z in range(3):
+                    b = 6 * (s0 - c0)
+                    if kind == "A":
+                        og, oh = B(P, b + 2 * z, b + 6 * n, 6), B(P, b + 2 * z + 1, b + 6 * n, 6)
+                    else:
+                        og, oh = B(P, b + z, b + 3 * n, 3), B(P, b + 3 * n + z, b + 6 * n, 3)
+                    mm(og, B("I"), B("c4096", 0, n), True, False)
+                    mm(og, B("TRI"), rc(z, s0, s1), False, True)
+                    mm(oh, B("I"), B("c4096", 0, n), True, False)
+                    mm(oh, B("BLK"), ro(s0, s1), False, False)
+                    mm(oh, B("TMO"), rc(z, s0, s1), False, True)
+            n = 6 * (c1 - c0)
+            va, vb = ("v1a", "v2a") if ci % 2 == 0 else ("v1b", "v2b")
+            tt(B(va, 0, n), B(P, 0, n), B("odd", 6 * c0, 6 * c1), AL.mult)
+            ts(B(vb, 0, n), B(va, 0, n), 2, 4095, AL.arith_shift_right, AL.bitwise_and)
+            vcopy(B("off", 6 * c0, 6 * c1), B(vb, 0, n))
+        for ch in CHUNKS:
+            c0, c1 = ch[0][1], ch[-1][2]
+            for z in range(3):
+                for s0 in range(c0, c1, 64):
+                    s1 = min(c1, s0 + 64)
+                    o = B("psQ", 3 * (s0 - c0) + z, 3 * (s1 - c0), 3)
+                    mm(o, B("I"), B("cm127", 0, s1 - s0), True, False)
+                    mm(o, B("BLK"), ro(s0, s1), False, False)
+                    mm(o, B("IMO"), rc(z, s0, s1), False, True)
+            ts(B("pen", 3 * c0, 3 * c1), B("psQ", 0, 3 * (c1 - c0)), MAGIC, MAGIC, AL.add, AL.not_equal)
+        vtrans(B("T12"), B("nX"))
+        n0, n1, n2 = B(nown[0]), B("T12", 0, 256, 16), B("T12", 256, 512, 16)
+        tt(B("dn1"), n1, n0, AL.subtract)
+        tt(B("dn2"), n2, n1, AL.subtract)
+        for s in range(SA):
+            o, of, bi = B("A", 96 * s, 96 * s + 96), B("off", 6 * s, 6 * s + 6), B("nobs", s, s + 1)
+            op("a", lambda e: e.activation(o[0], ind(B("S"), of), AF.Abs, bias=bi[0]), [B("S"), of, bi], [o])
+
+        def gat(b):
+            s0, s1 = DBLK[b]
+            n, base = 48 * (s1 - s0), 96 * (s0 - SA)
+            for gh in range(2):
+                lo = base + gh * n
+                c = 6 * s0 + gh * 3 * (s1 - s0)
+                of, x, o = B("off", c, c + 3 * (s1 - s0)), B("Xe", 48 * (s0 - SA), 48 * (s1 - SA)), B("dd", lo, lo + n)
+                op("v", lambda e: e.tensor_tensor(o[0], ind(B("S"), of), x[0], AL.subtract), [B("S"), of, x], [o])
+                ts(B("rr", lo, lo + n), o, 0.0, -2.0, AL.min, AL.mult)
+
+        def sums(name):
+            kind, b = name[0], int(name[1:])
+            s0, s1 = (ABLK if kind == "A" else DBLK)[b]
+            kb = [x for x in KEYBANK if x[0] <= s0 and s1 <= x[1]][0]
+            o, n = B(kb[2], 3 * (s0 - kb[0]), 3 * (s1 - kb[0])), 3 * (s1 - s0)
+            mm(o, B("I"), B("KC", 0, n), True, False)
+            mm(o, B("BIGI"), B("pen", 3 * s0, 3 * s1), False, False)
+            todo = []
+            for gh in range(2):
+                for k in range(15 + gh):
+                    wt = weight(gh, k)
+                    if kind == "A":
+                        todo.append((wt, B("A", 96 * s0 + 16 * gh + k, 96 * s1, 32)))
+                    else:
+                        lo = 96 * (s0 - SA) + gh * 16 * n
+                        todo.append((wt, B("dd", lo + k, lo + 16 * n, 16)))
+                if kind == "D":
+                    for k in range(15 + gh):
+                        wt = weight(gh, k)
+                        lo = 96 * (s0 - SA) + gh * 16 * n
+                        todo.append((wt, B("rr", lo + k, lo + 16 * n, 16)))
+            for i, (wt, r) in enumerate(todo):
+                mm(o, wt, r, False, i == len(todo) - 1)
+
+        def best1(lo, hi, ps, p0):
+            scan(B("z1", 3 * lo, 3 * hi), B("RS3", 0, 3 * (hi - lo)), B(ps, p0, p0 + 3 * (hi - lo)))
+
+        def best2(lo, hi):
+            vtrans(B("tr", lo, hi), B("z1", 3 * lo + 2, 3 * hi, 3))
+            scan(B("s2", lo, hi), B("RS16", 0, hi - lo), B("tr", lo, hi))
+
+        gat(0)
+        gat(1)
+        gat(2)
+        for nm in ORDER[:5]:
+            sums(nm)
+        best1(0, 96, "psKA", 0)
+        best2(0, 96)
+        gat(3)
+        for nm in ORDER[5:]:
+            sums(nm)
+        best1(144, 256, "psKC", 0)
+        best1(96, 144, "psKB", 0)
+        best2(96, 256)
+        last = t == NR - 1
+        bi, acc = B("s2", 15, 256, 16), B("acc%d" % t, 0, 16)
+        ts(B("sc"), bi, 6, None, AL.logical_shift_right)
+        ts(B("z16"), bi, 48, None, AL.bitwise_and)
+        ts(B("st"), bi, 15, None, AL.bitwise_and)
+        tt(acc, B("sc"), B("thr"), AL.is_lt)
+        tt(B("SWa", 0, 16), B("z16"), acc, AL.mult)
+        tt(B("SWa", 16, 32), B("st"), acc, AL.mult)
+        swap(("SWa", 0), 0, "ilist", "E16")
+        swap(("SWa", 16), 16)
+        ts(B("e2"), B("z16"), 32.0, None, AL.is_ge)
+        ts(B("e3"), B("z16"), 48.0, None, AL.is_ge)
+        tt(B("t2"), B("e2"), B("dn1"), AL.mult)
+        tt(B("t3"), B("e3"), B("dn2"), AL.mult)
+        tt(B("b1"), n0, B("t2"), AL.add)
+        vcopy(B("offB"), B("psS", 0, 32))
+        agather(B("Rb"), B(w, 32, 1056), B("offB", 0, 16))
+        vgather(B("OH"), B("ZI"), B("offB", 16, 32))
+        mm(B("psD", 0, 256), B("BLK"), ro(0, 256), True, False)
+        mm(B("psD", 0, 256), B("NBLK"), B("Rb"), False, True)
+        mm(B("psD", 256, 512), B("I"), B("Rb"), True, True)
+        tt(B("bn"), B("b1"), B("t3"), AL.add)
+        if not last:
+            wn = W[t + 1]
+            own = B(w, 16, 32)
+            tt(B("d1"), B("bn"), own, AL.subtract)
+            tt(B("d2"), B("d1"), acc, AL.mult)
+            tt(B(wn, 16, 32), B("d2"), own, AL.add)
+            swap((wn, 16), 32)
+        tt(B("md"), B("psD", 0, 256), B("OH"), AL.mult)
+        if not last:
+            tt(B(wn, 32, 288), B("psD", 256, 512), B("md"), AL.add)
+            vcopy(B(wn, 0, 16), B("psS", 32, 48))
+            send(t + 1)
+        else:
+            tt(B("Rf"), B("psD", 256, 512), B("md"), AL.add)
+            op("s", lambda e: e.dma_start(T.yr[:], T.Rf[:]), [B("Rf")], [], sem="st0", inc=16)
+        ts(B("h1"), B("bn"), 13.0, None, AL.mult)
+        tt(B("h2"), B("h1"), B("sc"), AL.add)
+        ts(B("h3"), B("h2"), 255, None, AL.bitwise_and)
+        tt(B("d3"), B("h3"), n2, AL.subtract)
+        tt(B("d4"), B("d3"), acc, AL.mult)
+        tt(B("d5"), B("sc"), B("F"), AL.subtract)
+        tt(B("d6"), B("d5"), acc, AL.mult)
+        if not last:
+            nn = "nL" if nown[0] == "nLn" else "nLn"
+            tt(B(nn), B("d4"), n2, AL.add)
+            swap((nn, 0), 48)
+            nown[0] = nn
+            tt(B("F"), B("d6"), B("F"), AL.add)
+            vcopy(B("n0U"), B("psS", 48, 64))
+            vcopy(B("acc%d" % t, 16, 32), acc)
+            k = 0
+            for r in range(t + 1):
+                for s in range(8):
+                    mm(B("psS", 64, 80), B("BLK32"), B("acc%d" % r, 2 * s, 2 * s + 16), k == 0, k == 8 * (t + 1) - 1)
+                    k += 1
+            vcopy(B("Ai"), B("psS", 64, 80))
+            ts(B("A7"), B("Ai"), 7, None, AL.bitwise_and)
+            tt(B("thr"), B("F"), B("A7"), AL.subtract)
+        else:
+            memset(B("B2"), 0.0)
+            tt(B("B2", 0, 256, 16), B("d6"), B("F"), AL.add)
+            tt(B("B2", 1, 256, 16), B("d4"), n2, AL.add)
+            vtrans(B("oT"), B("B2"))
+            op("s", lambda e: e.dma_start(T.yf[:], T.oT[0:128:16, :]), [B("oT")], [], sem="st1", inc=16)
+            op("a", lambda e: e.dma_start(T.yn[:], T.oT[1:128:16, :]), [B("oT")], [], sem="st2", inc=16)
+    for s in sorted(total):
+        if known["g"].get(s, 0) < total[s]:
+            g.wait_ge(T.sem[s], total[s])

@@ -6,59 +6,55 @@ AL = AluOpType
 AF = ActivationFunctionType
 NR = 3
 V = 256
-SA = 144
-ABLK = [(0, 32), (32, 64), (64, 96), (96, 128), (128, 144)]
-DBLK = [(144, 176), (176, 208), (208, 240), (240, 256)]
-CHUNKS = [[("A", 0, 32)], [("A", 32, 96)], [("A", 96, 144)],
-          [("D", 144, 176), ("D", 176, 208)], [("D", 208, 240), ("D", 240, 256)]]
-ORDER = ["A0", "D0", "A1", "D1", "A2", "D2", "A3", "D3", "A4"]
-KEYBANK = [(0, 96, "psKA"), (96, 144, "psKB"), (144, 256, "psKC")]
-PAY = 288
+DS, DE = 16, 130
+NA, ND = DS + V - DE, DE - DS
+ABLK = [(DE + (V - DE) * i // 4, DE + (V - DE) * (i + 1) // 4) for i in range(4)]
+ALATE = (0, DS)
+DBLK = [(32, 64), (64, 96), (96, DE)]
+DLATE = (DS, 32)
+CHUNKS = [[("A", DE, DE + 16)], [("A", DE + 16, DE + 80)], [("A", DE + 80, V)],
+          [("D", 32, 64), ("D", 64, 96)], [("D", 96, DE)], [("A", 0, DS), ("D", DS, 32)]]
+ORDER = ["A0", "D0", "A1", "D1", "A2", "D2", "A3"]
+KEYBANK = [(0, 32, "psKB"), (32, DE, "psKC"), (DE, V, "psKA")]
+PAY = 272
+CUT = 1024
 BIG = 33554432.0
 MAGIC = 1.5 * 2.0 ** 31
 
+
+def sb(cols, kind="bfloat16"):
+    return ("sbuf", [128, cols], kind)
+
+
 SCRATCH = {
-    "S": ("sbuf", [128, 4096], "bfloat16"), "obs_s": ("sbuf", [128, 256], "bfloat16"), "nobs": ("sbuf", [128, 256], "float32"),
-    "Xe": ("sbuf", [128, (V - SA) * 48], "bfloat16"),
-    "rawR": ("sbuf", [128, 256], "int32"), "raws": ("sbuf", [128, 16], "int32"), "rawn": ("sbuf", [128, 16], "int32"),
-    "fitb": ("sbuf", [128, 256], "int32"), "fitf": ("sbuf", [128, 256], "float32"), "fitt": ("sbuf", [128, 256], "float32"),
-    "W0": ("sbuf", [128, 1056], "bfloat16"), "W1": ("sbuf", [128, 1056], "bfloat16"), "W2": ("sbuf", [128, 1056], "bfloat16"),
-    "land0": ("sbuf", [128, PAY], "bfloat16"), "land1": ("sbuf", [128, PAY], "bfloat16"), "land2": ("sbuf", [128, PAY], "bfloat16"),
-    "LQ1": ("sbuf", [128, 256], "bfloat16"), "LQ2": ("sbuf", [128, 256], "bfloat16"),
-    "srcU": ("sbuf", [128, 16], "uint16"), "n0U": ("sbuf", [128, 16], "uint16"), "offB": ("sbuf", [128, 32], "uint16"),
-    "B1": ("sbuf", [128, 256], "bfloat16"), "X": ("sbuf", [128, 256], "bfloat16"), "X2": ("sbuf", [128, 256], "bfloat16"),
-    "nX": ("sbuf", [128, 512], "bfloat16"), "T12": ("sbuf", [128, 512], "bfloat16"),
-    "off": ("sbuf", [128, 1536], "uint16"), "odd": ("sbuf", [128, 1536], "float32"),
-    "v1a": ("sbuf", [128, 384], "int32"), "v1b": ("sbuf", [128, 384], "int32"), "v2a": ("sbuf", [128, 384], "int32"), "v2b": ("sbuf", [128, 384], "int32"),
-    "pen": ("sbuf", [128, 768], "bfloat16"),
-    "A": ("sbuf", [128, SA * 96], "bfloat16"), "dd": ("sbuf", [128, (V - SA) * 96], "bfloat16"), "rr": ("sbuf", [128, (V - SA) * 96], "bfloat16"),
-    "z1": ("sbuf", [128, 768], "float32"), "tr": ("sbuf", [128, 256], "float32"), "s2": ("sbuf", [128, 256], "int32"),
-    "sc": ("sbuf", [128, 16], "int32"), "z16": ("sbuf", [128, 16], "int32"), "st": ("sbuf", [128, 16], "int32"),
-    "acc0": ("sbuf", [128, 32], "bfloat16"), "acc1": ("sbuf", [128, 32], "bfloat16"), "acc2": ("sbuf", [128, 32], "bfloat16"),
-    "SWa": ("sbuf", [128, 32], "bfloat16"), "nL": ("sbuf", [128, 16], "bfloat16"), "nLn": ("sbuf", [128, 16], "bfloat16"), "srcb": ("sbuf", [128, 16], "bfloat16"),
-    "F": ("sbuf", [128, 16], "float32"), "thr": ("sbuf", [128, 16], "float32"), "Ai": ("sbuf", [128, 16], "int32"), "A7": ("sbuf", [128, 16], "int32"),
-    "dn1": ("sbuf", [128, 16], "float32"), "dn2": ("sbuf", [128, 16], "float32"),
-    "e2": ("sbuf", [128, 16], "float32"), "e3": ("sbuf", [128, 16], "float32"), "t2": ("sbuf", [128, 16], "float32"), "t3": ("sbuf", [128, 16], "float32"),
-    "b1": ("sbuf", [128, 16], "float32"), "bn": ("sbuf", [128, 16], "float32"), "d1": ("sbuf", [128, 16], "float32"), "d2": ("sbuf", [128, 16], "float32"),
-    "h1": ("sbuf", [128, 16], "float32"), "h2": ("sbuf", [128, 16], "int32"), "h3": ("sbuf", [128, 16], "int32"), "d3": ("sbuf", [128, 16], "float32"), "d4": ("sbuf", [128, 16], "float32"),
-    "d5": ("sbuf", [128, 16], "float32"), "d6": ("sbuf", [128, 16], "float32"),
-    "Rb": ("sbuf", [128, 256], "bfloat16"), "OH": ("sbuf", [128, 256], "bfloat16"), "md": ("sbuf", [128, 256], "bfloat16"),
-    "Rf": ("sbuf", [128, 256], "float32"), "B2": ("sbuf", [128, 256], "float32"), "oT": ("sbuf", [128, 256], "float32"),
-    "ones": ("sbuf", [128, 128], "bfloat16"), "I": ("sbuf", [128, 128], "bfloat16"), "BLK": ("sbuf", [128, 128], "bfloat16"), "TRI": ("sbuf", [128, 128], "bfloat16"),
-    "TMO": ("sbuf", [128, 128], "bfloat16"), "IMO": ("sbuf", [128, 128], "bfloat16"), "NBLK": ("sbuf", [128, 128], "bfloat16"), "BIGI": ("sbuf", [128, 128], "bfloat16"),
-    "BLK32": ("sbuf", [128, 128], "bfloat16"), "B48": ("sbuf", [128, 8, 48], "bfloat16"), "WT": ("sbuf", [128, 248, 16], "bfloat16"),
-    "E": ("sbuf", [128, 512], "bfloat16"), "E16": ("sbuf", [128, 512], "bfloat16"),
-    "c4096": ("sbuf", [128, 64], "bfloat16"), "cm127": ("sbuf", [128, 64], "bfloat16"),
-    "pi": ("sbuf", [128, 1], "int32"), "pj": ("sbuf", [128, 1], "int32"), "jcol": ("sbuf", [128, 1], "float32"),
-    "kct": ("sbuf", [128, 96], "float32"), "KC": ("sbuf", [128, 96], "bfloat16"),
-    "ilt": ("sbuf", [128, 16], "float32"), "ilist": ("sbuf", [128, 16], "bfloat16"), "zit": ("sbuf", [128, 16], "float32"), "ZI": ("sbuf", [128, 16], "bfloat16"),
-    "RS3": ("sbuf", [128, 336], "float32"), "RS16": ("sbuf", [128, 256], "float32"),
+    "S": sb(4096), "obs_s": sb(256), "nobs": sb(256, "float32"), "Xe": sb(ND * 48),
+    "rawR": sb(256, "int32"), "raws": sb(16, "int32"), "rawn": sb(16, "int32"),
+    "fitb": sb(256, "int32"), "fitf": sb(256, "float32"), "fitt": sb(256, "float32"),
+    "W0": sb(1040), "W1": sb(1040), "W2": sb(1040), "land0": sb(PAY), "land1": sb(PAY), "land2": sb(PAY),
+    "LQ1": sb(256), "LQ2": sb(256), "srcU": sb(16, "uint16"), "n0U": sb(16, "uint16"), "offB": sb(32, "uint16"),
+    "B1": sb(256), "X": sb(256), "X2": sb(256), "nX": sb(512), "T12": sb(512),
+    "off": sb(1536, "uint16"), "odd": sb(1536, "float32"),
+    "v1a": sb(384, "int32"), "v1b": sb(384, "int32"), "v2a": sb(384, "int32"), "v2b": sb(384, "int32"),
+    "pen": sb(768), "A": sb(NA * 96), "dd": sb(ND * 96), "rr": sb(ND * 96),
+    "z1": sb(768, "float32"), "tr": sb(256, "float32"), "s2": sb(256, "int32"),
+    "sc": sb(16, "int32"), "z16": sb(16, "int32"), "st": sb(16, "int32"), "SWa": sb(32),
+    "acc0": sb(32), "acc1": sb(32), "IND": sb(48), "PQ": sb(48), "TP": sb(48),
+    "nL": sb(16), "nLn": sb(16), "srcA": sb(16), "srcB": sb(16),
+    "F": sb(16, "float32"), "thr": sb(16, "float32"), "Ai": sb(16, "int32"), "A7": sb(16, "int32"),
+    "b1": sb(16, "float32"), "bn": sb(16, "float32"), "h1": sb(16, "float32"), "h2": sb(16, "int32"), "h3": sb(16, "int32"),
+    "d3": sb(16, "float32"), "d4": sb(16, "float32"), "d5": sb(16, "float32"), "d6": sb(16, "float32"),
+    "Rb": sb(256), "OH": sb(256), "md": sb(256), "Rf": sb(256, "float32"), "B2": sb(256, "float32"), "oT": sb(256, "float32"),
+    "ones": sb(128), "I": sb(128), "BLK": sb(128), "TRI": sb(128), "TMO": sb(128), "IMO": sb(128), "NBLK": sb(128), "BIGI": sb(128),
+    "BLK32": sb(128), "B48": ("sbuf", [128, 8, 48], "bfloat16"), "WT": ("sbuf", [128, 248, 16], "bfloat16"), "E": sb(512), "E16": sb(512),
+    "c4096": sb(64), "cm127": sb(160), "pi": sb(1, "int32"), "pj": sb(1, "int32"), "jcol": sb(1, "float32"),
+    "kct": sb(120, "float32"), "KC": sb(120), "ilt": sb(16, "float32"), "ilist": sb(16), "zit": sb(16, "float32"), "ZI": sb(16),
+    "RS3": sb(420, "float32"), "RS16": sb(256, "float32"),
     "psP0": ("psum", [128, 512], "float32"), "psP1": ("psum", [128, 512], "float32"), "psQ": ("psum", [128, 512], "float32"),
     "psKA": ("psum", [128, 512], "float32"), "psKB": ("psum", [128, 512], "float32"), "psKC": ("psum", [128, 512], "float32"),
     "psS": ("psum", [128, 512], "float32"), "psD": ("psum", [128, 512], "float32"),
 }
-SEMAPHORES = (["qv", "qa", "qp", "qg"] + ["ld%d" % i for i in range(6)] + ["st%d" % i for i in range(3)]
-              + ["%s%d" % (n, t) for n in ("arr", "hop", "loc", "hl") for t in range(NR)])
+SEMAPHORES = (["qv", "qa", "qp", "qg", "go", "ldf"] + ["ld%d" % i for i in range(6)] + ["st%d" % i for i in range(4)]
+              + ["%s%s%d" % (n, p, t) for n in ("arr", "hop", "loc", "hl") for t in range(NR) for p in "EL"])
 
 
 def route(q, t, cores, topo):
@@ -77,7 +73,12 @@ def pick(src, dst, topo):
     return sum(1 << i for i in e), len(e)
 
 
+def pieces(t):
+    return [("L", 0, 16), ("E", 16, PAY)] if t == 0 else [("E", 0, PAY)]
+
+
 def relay_program(g, core, T, topo):
+    held = []
     for t in range(NR):
         for q in range(len(T.cores)):
             dst, via = route(q, t, T.cores, topo)
@@ -86,15 +87,14 @@ def relay_program(g, core, T, topo):
             _, n1 = pick(T.cores[q], core, topo)
             m, n2 = pick(core, dst, topo)
             rid, pid = topo.addr(dst, core)
-            land = T["land%d" % t]
-            g.wait_ge(T.sem["hop%d" % t], n1)
-            g.remote_dma(out_ap=land[:], in_ap=land[:], remote_sem=T.sem["arr%d" % t], local_sem=T.sem["hl%d" % t],
-                         pid=pid, routing_id=rid, dma_engine_mask=m)
-    for t in range(NR):
-        for q in range(len(T.cores)):
-            dst, via = route(q, t, T.cores, topo)
-            if via == core:
-                g.wait_ge(T.sem["hl%d" % t], pick(core, dst, topo)[1])
+            for p, a, b in pieces(t):
+                land = T["land%d" % t][:, a:b]
+                g.wait_ge(T.sem["hop%s%d" % (p, t)], n1)
+                g.remote_dma(out_ap=land, in_ap=land, remote_sem=T.sem["arr%s%d" % (p, t)], local_sem=T.sem["hl%s%d" % (p, t)],
+                             pid=pid, routing_id=rid, dma_engine_mask=m)
+                held.append(("hl%s%d" % (p, t), n2))
+    for s, n in held:
+        g.wait_ge(T.sem[s], n)
 
 
 def rank_program(g, core, T, topo):
@@ -141,21 +141,16 @@ def rank_program(g, core, T, topo):
         s = "q" + q if own else sem
         tag = q if own else "x" + sem
         want = {}
-        for v in reads:
+        for v in reads + writes:
             if v[1][:2] == "ps":
                 for a, tok in bank.get(v[1], {}).items():
                     if a != tag:
                         need(want, tok)
-                continue
+        for v in reads:
             for r in rec.get(v[1], []):
                 if r[0] == "w" and clash(r, v):
                     need(want, r[4])
         for v in writes:
-            if v[1][:2] == "ps":
-                for a, tok in bank.get(v[1], {}).items():
-                    if a != tag:
-                        need(want, tok)
-                continue
             for r in rec.get(v[1], []):
                 if (r[3] != tag or r[0] == "w") and clash(r, v):
                     need(want, r[4])
@@ -206,6 +201,9 @@ def rank_program(g, core, T, topo):
     def vcopy(out, a):
         return op("v", lambda e: e.tensor_copy(out[0], a[0]), [a], [out])
 
+    def acopy(out, a):
+        return op("a", lambda e: e.activation(out[0], a[0], AF.Copy), [a], [out])
+
     def vgather(out, win, of):
         return op("v", lambda e: e.tensor_copy(out[0], ind(win, of)), [win, of], [out])
 
@@ -229,6 +227,9 @@ def rank_program(g, core, T, topo):
         nload[0] += 1
         return op(q, lambda e: e.dma_start(out[0], src), [], [out], sem="ld%d" % k, inc=16)
 
+    def store(q, out, src, sem):
+        return op(q, lambda e: e.dma_start(out, src[0]), [src], [], sem=sem, inc=16)
+
     def iota(out, pattern, base, cm, f=True):
         if f:
             return op("g", lambda e: e.iota(out[0], pattern, base, cm, allow_small_or_imprecise_dtypes=True), [], [out])
@@ -237,32 +238,32 @@ def rank_program(g, core, T, topo):
     def sel(out, a, pattern, cmp, base, cm):
         return op("g", lambda e: e.affine_select(out[0], a[0], pattern, cmp, 0.0, base, cm), [a], [out])
 
+    def apos(s):
+        return s if s < DS else s - ND
+
     def weight(gh, k):
         n = 15 * gh + k
         return (T.WT[:, 8 * n:8 * n + 8, :], "WT", n, n + 1)
 
     def put_weight(gh, k, q):
         lo = 15 - k if gh == 0 else 31 - k
-        i, o = (T.B48[:, :, lo:lo + 16], "B48", 0, 384), weight(gh, k)
-        if q == "v":
-            return vcopy(o, i)
-        return op("a", lambda e: e.activation(o[0], i[0], AF.Copy), [i], [o])
+        (vcopy if q == "v" else acopy)(weight(gh, k), (T.B48[:, :, lo:lo + 16], "B48", 0, 384))
 
-    def swap(field, col, extra=None, name="E"):
+    def swap(field, col, extra=None, name="E", a=0, b=16):
         fb, fo = field
         for h in range(2):
-            o = B("psS", col + h, col + 16, 2)
+            o = B("psS", col + a + h, col + b, 2)
             if extra is not None:
-                mm(o, B("I"), B(extra, h, 16, 2), True, False)
+                mm(o, B("I"), B(extra, a + h, b, 2), True, False)
             for e in range(2):
                 k = 128 * (2 * e + h)
-                mm(o, B(name, k, k + 128), B(fb, fo + e, fo + 16, 2), extra is None and e == 0, e == 1)
+                mm(o, B(name, k, k + 128), B(fb, fo + a + e, fo + b, 2), extra is None and e == 0, e == 1)
 
     W = ["W0", "W1", "W2"]
     load("s", B("rawR"), T.resid[:])
     load("a", B("raws"), T.src0[:])
     load("a", B("rawn"), T.nx0[:])
-    load("s", B("S"), T.prof[:])
+    load("s", B("S", 0, CUT), T.prof[:, 0:CUT])
     load("a", B("obs_s"), T.obs[:])
     memset(B("ones"), 1.0)
     memset(B("E"), 0.0)
@@ -270,58 +271,67 @@ def rank_program(g, core, T, topo):
     op("v", lambda e: e.memset(T.B48[:, :, 0:16], 0.0), [], [("", "B48", 0, 384)])
     op("v", lambda e: e.memset(T.B48[:, :, 16:32], 64.0), [], [("", "B48", 0, 384)])
     op("v", lambda e: e.memset(T.B48[:, :, 32:48], 0.0), [], [("", "B48", 0, 384)])
-    op("a", lambda e: e.dma_start(T.fitb[0:128:16, :], T.fit0[:]), [], [B("fitb")], sem="ld5", inc=16)
+    op("a", lambda e: e.dma_start(T.fitb[0:128:16, :], T.fit0[:]), [], [B("fitb")], sem="ldf", inc=16)
     iota(B("pi"), [[0, 1]], 0, 1, False)
     sel(B("I"), B("ones"), [[-1, 128]], AL.is_equal, 0, 1)
     iota(B("ilt"), [[16, 16]], 0, 0)
     iota(B("zit"), [[1, 16]], 0, 0)
-    iota(B("kct"), [[0, 32], [16, 3]], 16, 0)
+    sel(B("BLK"), B("ones"), [[-16, 8], [0, 16]], AL.is_ge, 0, 1)
+    sel(B("BLK"), B("BLK"), [[16, 8], [0, 16]], AL.is_ge, 15, -1)
+    memset(B("RS3"), 0.0)
+    memset(B("RS3", 0, 420, 3), BIG)
+    vcopy(B("W0", 0, 16), B("raws"))
+    vcopy(B("W0", 16, PAY), B("rawR"))
+
+    def send(t, piece):
+        p, a, b = piece
+        dst, via = route(rank, t, T.cores, topo)
+        to = dst if via is None else via
+        m, n = pick(core, to, topo)
+        rid, pid = topo.addr(to, core)
+        rs, ls = T.sem["%s%s%d" % ("arr" if via is None else "hop", p, t)], "loc%s%d" % (p, t)
+        src = B(W[t], a, b)
+        op("g", lambda e: e.remote_dma(out_ap=T["land%d" % t][:, a:b], in_ap=src[0], remote_sem=rs, local_sem=T.sem[ls],
+                                       pid=pid, routing_id=rid, dma_engine_mask=m), [src], [], sem=ls, inc=n, then=False)
+
+    def expect(t):
+        for q in range(len(T.cores)):
+            dst, via = route(q, t, T.cores, topo)
+            if dst == core:
+                for p, a, b in pieces(t):
+                    arrived("land%d" % t, a, b, "arr%s%d" % (p, t), pick(T.cores[q] if via is None else via, core, topo)[1])
+
+    for piece in pieces(0):
+        send(0, piece)
+    g.sem_inc(T.sem["go"], 1)
+    total["go"] = 1
+    g.sync.wait_ge(T.sem["go"], 1)
+    load("s", B("S", CUT, 4096), T.prof[:, CUT:4096])
+    sel(B("TRI"), B("BLK"), [[1, 128]], AL.is_ge, 0, -1)
+    iota(B("kct"), [[0, 40], [16, 3]], 16, 0)
+    b48 = (T.B48[:], "B48", 0, 384)
+    sel(b48, b48, [[-16, 8], [0, 48]], AL.is_ge, 0, 1)
+    sel(b48, b48, [[16, 8], [0, 48]], AL.is_ge, 15, -1)
+    iota(B("odd", 6 * DE, 1536), [[2, V - DE], [0, 6]], 2 * DE + 1, 0)
+    iota(B("odd", 0, 6 * DS), [[2, DS], [0, 6]], 1, 0)
+    for s0, s1 in DBLK + [DLATE]:
+        iota(B("odd", 6 * s0, 6 * s1), [[0, 2], [2, s1 - s0], [0, 3]], 2 * s0 + 1, 0)
+    sel(B("BLK32"), B("ones"), [[-32, 4], [0, 32]], AL.is_ge, 0, 1)
+    sel(B("BLK32"), B("BLK32"), [[32, 4], [0, 32]], AL.is_ge, 31, -1)
     for e in range(2):
         for h in range(2):
             for a in range(4):
                 k = 128 * (2 * e + h) + 32 * a
                 vcopy(B("E", k + 16 * e, k + 16 * e + 16), B("I", 32 * a + 16 * h, 32 * a + 16 * h + 16))
     ts(B("E16"), B("E"), 16.0, None, AL.mult)
-    vcopy(B("W0", 0, 16), B("raws"))
-    swap(("W0", 0), 0)
-    vcopy(B("W0", 16, 32), B("psS", 0, 16))
-    vcopy(B("W0", 32, 288), B("rawR"))
-    sel(B("BLK"), B("ones"), [[-16, 8], [0, 16]], AL.is_ge, 0, 1)
-    sel(B("BLK"), B("BLK"), [[16, 8], [0, 16]], AL.is_ge, 15, -1)
-    sel(B("TRI"), B("BLK"), [[1, 128]], AL.is_ge, 0, -1)
-
-    def send(t):
-        dst, via = route(rank, t, T.cores, topo)
-        to = dst if via is None else via
-        m, n = pick(core, to, topo)
-        rid, pid = topo.addr(to, core)
-        rs = T.sem[("arr%d" if via is None else "hop%d") % t]
-        src = B(W[t], 0, PAY)
-        op("g", lambda e: e.remote_dma(out_ap=T["land%d" % t][:], in_ap=src[0], remote_sem=rs, local_sem=T.sem["loc%d" % t],
-                                       pid=pid, routing_id=rid, dma_engine_mask=m), [src], [], sem="loc%d" % t, inc=n, then=False)
-
-    def expect(t):
-        for q in range(len(T.cores)):
-            dst, via = route(q, t, T.cores, topo)
-            if dst == core:
-                arrived("land%d" % t, 0, PAY, "arr%d" % t, pick(T.cores[q] if via is None else via, core, topo)[1])
-
-    send(0)
-    b48 = (T.B48[:], "B48", 0, 384)
-    sel(b48, b48, [[-16, 8], [0, 48]], AL.is_ge, 0, 1)
-    sel(b48, b48, [[16, 8], [0, 48]], AL.is_ge, 15, -1)
-    iota(B("odd", 0, 6 * SA), [[2, SA], [0, 6]], 1, 0)
-    for s0, s1 in DBLK:
-        iota(B("odd", 6 * s0, 6 * s1), [[0, 2], [2, s1 - s0], [0, 3]], 2 * s0 + 1, 0)
-    sel(B("BLK32"), B("ones"), [[-32, 4], [0, 32]], AL.is_ge, 0, 1)
-    sel(B("BLK32"), B("BLK32"), [[32, 4], [0, 32]], AL.is_ge, 31, -1)
     vcopy(B("nL"), B("rawn"))
     swap(("nL", 0), 32)
+    swap(("W0", 0), 48)
     vcopy(B("n0U"), B("rawn"))
     vcopy(B("nLn"), B("psS", 32, 48))
+    vcopy(B("srcA"), B("psS", 48, 64))
     ts(B("pj"), B("pi"), 15, None, AL.bitwise_and)
     vcopy(B("jcol"), B("pj"))
-    ts(B("KC"), B("kct"), None, None, AL.add, col=B("jcol"))
     ts(B("ilist"), B("ilt"), None, None, AL.add, col=B("jcol"))
     ts(B("ZI"), B("zit"), None, None, AL.is_equal, col=B("jcol"))
     memset(B("c4096"), 4096.0)
@@ -331,47 +341,50 @@ def rank_program(g, core, T, topo):
     ts(B("NBLK"), B("BLK"), -1.0, None, AL.mult)
     ts(B("BIGI"), B("I"), 4194304.0, None, AL.mult)
     memset(B("B1"), 0.0)
-    memset(B("RS3"), 0.0)
-    memset(B("RS3", 0, 336, 3), BIG)
+    memset(B("B2"), 0.0)
     memset(B("RS16"), 0.0)
     memset(B("RS16", 0, 256, 16), BIG)
     ts(B("nobs"), B("obs_s"), -1.0, None, AL.mult)
     for k in range(48):
-        o, i = B("Xe", k, (V - SA) * 48, 48), B("obs_s", SA, V)
-        if k % 2:
-            op("a", lambda e: e.activation(o[0], i[0], AF.Copy), [i], [o])
-        else:
-            vcopy(o, i)
+        (acopy if k % 2 else vcopy)(B("Xe", k, ND * 48, 48), B("obs_s", DS, DE))
     for gh in range(2):
         for k in range(15 + gh):
             put_weight(gh, k, "a" if k % 2 else "v")
+    ts(B("KC"), B("kct"), None, None, AL.add, col=B("jcol"))
     vcopy(B("fitf"), B("fitb"))
     vtrans(B("fitt"), B("fitf"))
     vcopy(B("F"), B("fitt", 0, 256, 16))
-    vcopy(B("thr"), B("F"))
+    ts(B("thr"), B("F"), 64.0, None, AL.mult)
 
-    nown = ["nLn"]
+    nown, sown = ["nLn", "nL"], ["srcA", "srcB"]
     for t in range(NR):
-        w, land = W[t], "land%d" % t
+        w, land, last = W[t], "land%d" % t, t == NR - 1
+        wn = None if last else W[t + 1]
         expect(t)
 
-        def ro(a, b, w=w):
-            return B(w, 32 + a, 32 + b)
+        def ro(a, b):
+            return B(w, 16 + a, 16 + b)
 
-        def rc(z, a, b, w=w):
-            return B(w, 32 + 256 * (z + 1) + a, 32 + 256 * (z + 1) + b)
-        lists = B(land, 32, 288)
+        def rc(z, a, b):
+            return B(w, 16 + 256 * (z + 1) + a, 16 + 256 * (z + 1) + b)
+
+        lists = B(land, 16, PAY)
+        f0 = 2 * (DE // 32)
+        rest = [(0, f0), (f0 + 4, 16)]
+
+        def nx(c0, c1):
+            return B("n0U", c0, c1)
         vcopy(B("srcU"), B(land, 0, 16))
-        agather(B("LQ1"), lists, B("srcU"))
-        vgather(rc(0, 0, 256), lists, B("n0U"))
-        agather(B("LQ2"), B("LQ1"), B("srcU"))
-        vgather(rc(1, 0, 256), B("LQ1"), B("n0U"))
-        vgather(rc(2, 0, 256), B("LQ2"), B("n0U"))
-        vcopy(B("B1", 0, 256, 16), B(land, 16, 32))
-        vtrans(B("X"), B("B1"))
-        agather(B("X2"), B("X"), B("srcU"))
-        agather(B("nX", 0, 256), B("X"), B("n0U"))
-        agather(B("nX", 256, 512), B("X2"), B("n0U"))
+        agather(B("LQ1", 0, 128), lists, B("srcU", 0, 8))
+        vgather(B("LQ1", 128, 256), lists, B("srcU", 8, 16))
+        vgather(rc(0, 16 * f0, 16 * f0 + 64), lists, nx(f0, f0 + 4))
+        agather(B("LQ2", 0, 128), B("LQ1"), B("srcU", 0, 8))
+        vgather(B("LQ2", 128, 256), B("LQ1"), B("srcU", 8, 16))
+        vgather(rc(1, 16 * f0, 16 * f0 + 64), B("LQ1"), nx(f0, f0 + 4))
+        vgather(rc(2, 16 * f0, 16 * f0 + 64), B("LQ2"), nx(f0, f0 + 4))
+        for c0, c1 in rest:
+            agather(rc(1, 16 * c0, 16 * c1), B("LQ1"), nx(c0, c1))
+            agather(rc(2, 16 * c0, 16 * c1), B("LQ2"), nx(c0, c1))
         for ci, ch in enumerate(CHUNKS):
             c0, c1 = ch[0][1], ch[-1][2]
             P = "psP%d" % (ci % 2)
@@ -393,130 +406,166 @@ def rank_program(g, core, T, topo):
             tt(B(va, 0, n), B(P, 0, n), B("odd", 6 * c0, 6 * c1), AL.mult)
             ts(B(vb, 0, n), B(va, 0, n), 2, 4095, AL.arith_shift_right, AL.bitwise_and)
             vcopy(B("off", 6 * c0, 6 * c1), B(vb, 0, n))
-        for ch in CHUNKS:
-            c0, c1 = ch[0][1], ch[-1][2]
+            if ci == 0:
+                for a, b in rest:
+                    vgather(rc(0, 16 * a, 16 * b), lists, nx(a, b))
+        for P, c0, c1 in (("psQ", DE, V), ("psP0", 32, DE), ("psP1", 0, 32)):
             for z in range(3):
-                for s0 in range(c0, c1, 64):
-                    s1 = min(c1, s0 + 64)
-                    o = B("psQ", 3 * (s0 - c0) + z, 3 * (s1 - c0), 3)
-                    mm(o, B("I"), B("cm127", 0, s1 - s0), True, False)
-                    mm(o, B("BLK"), ro(s0, s1), False, False)
-                    mm(o, B("IMO"), rc(z, s0, s1), False, True)
-            ts(B("pen", 3 * c0, 3 * c1), B("psQ", 0, 3 * (c1 - c0)), MAGIC, MAGIC, AL.add, AL.not_equal)
-        vtrans(B("T12"), B("nX"))
-        n0, n1, n2 = B(nown[0]), B("T12", 0, 256, 16), B("T12", 256, 512, 16)
-        tt(B("dn1"), n1, n0, AL.subtract)
-        tt(B("dn2"), n2, n1, AL.subtract)
-        for s in range(SA):
-            o, of, bi = B("A", 96 * s, 96 * s + 96), B("off", 6 * s, 6 * s + 6), B("nobs", s, s + 1)
-            op("a", lambda e: e.activation(o[0], ind(B("S"), of), AF.Abs, bias=bi[0]), [B("S"), of, bi], [o])
+                o = B(P, z, 3 * (c1 - c0), 3)
+                mm(o, B("I"), B("cm127", 0, c1 - c0), True, False)
+                mm(o, B("BLK"), ro(c0, c1), False, False)
+                mm(o, B("IMO"), rc(z, c0, c1), False, True)
+            ts(B("pen", 3 * c0, 3 * c1), B(P, 0, 3 * (c1 - c0)), MAGIC, MAGIC, AL.add, AL.not_equal)
+        swap((land, 0), 32)
+        n0, srcl = B(nown[0]), B(sown[0])
+        tt(B("PQ", 0, 16), n0, srcl, AL.subtract)
 
-        def gat(b):
-            s0, s1 = DBLK[b]
-            n, base = 48 * (s1 - s0), 96 * (s0 - SA)
+        def absd(s0, s1):
+            for s in range(s0, s1):
+                p = 96 * apos(s)
+                o, of, bi = B("A", p, p + 96), B("off", 6 * s, 6 * s + 6), B("nobs", s, s + 1)
+                op("a", lambda e: e.activation(o[0], ind(B("S"), of), AF.Abs, bias=bi[0]), [B("S"), of, bi], [o])
+
+        def gat(blk):
+            s0, s1 = blk
+            n, base = 48 * (s1 - s0), 96 * (s0 - DS)
             for gh in range(2):
                 lo = base + gh * n
                 c = 6 * s0 + gh * 3 * (s1 - s0)
-                of, x, o = B("off", c, c + 3 * (s1 - s0)), B("Xe", 48 * (s0 - SA), 48 * (s1 - SA)), B("dd", lo, lo + n)
+                of, x, o = B("off", c, c + 3 * (s1 - s0)), B("Xe", 48 * (s0 - DS), 48 * (s1 - DS)), B("dd", lo, lo + n)
                 op("v", lambda e: e.tensor_tensor(o[0], ind(B("S"), of), x[0], AL.subtract), [B("S"), of, x], [o])
                 ts(B("rr", lo, lo + n), o, 0.0, -2.0, AL.min, AL.mult)
 
-        def sums(name):
-            kind, b = name[0], int(name[1:])
-            s0, s1 = (ABLK if kind == "A" else DBLK)[b]
+        def sums(kind, blk):
+            s0, s1 = blk
             kb = [x for x in KEYBANK if x[0] <= s0 and s1 <= x[1]][0]
             o, n = B(kb[2], 3 * (s0 - kb[0]), 3 * (s1 - kb[0])), 3 * (s1 - s0)
             mm(o, B("I"), B("KC", 0, n), True, False)
             mm(o, B("BIGI"), B("pen", 3 * s0, 3 * s1), False, False)
             todo = []
             for gh in range(2):
-                for k in range(15 + gh):
-                    wt = weight(gh, k)
-                    if kind == "A":
-                        todo.append((wt, B("A", 96 * s0 + 16 * gh + k, 96 * s1, 32)))
-                    else:
-                        lo = 96 * (s0 - SA) + gh * 16 * n
-                        todo.append((wt, B("dd", lo + k, lo + 16 * n, 16)))
-                if kind == "D":
+                for buf in ("A",) if kind == "A" else ("dd", "rr"):
                     for k in range(15 + gh):
-                        wt = weight(gh, k)
-                        lo = 96 * (s0 - SA) + gh * 16 * n
-                        todo.append((wt, B("rr", lo + k, lo + 16 * n, 16)))
+                        if kind == "A":
+                            p = 96 * apos(s0)
+                            todo.append((weight(gh, k), B(buf, p + 16 * gh + k, p + 32 * n, 32)))
+                        else:
+                            lo = 96 * (s0 - DS) + gh * 16 * n
+                            todo.append((weight(gh, k), B(buf, lo + k, lo + 16 * n, 16)))
             for i, (wt, r) in enumerate(todo):
                 mm(o, wt, r, False, i == len(todo) - 1)
 
-        def best1(lo, hi, ps, p0):
-            scan(B("z1", 3 * lo, 3 * hi), B("RS3", 0, 3 * (hi - lo)), B(ps, p0, p0 + 3 * (hi - lo)))
+        def best1(lo, hi, ps):
+            scan(B("z1", 3 * lo, 3 * hi), B("RS3", 0, 3 * (hi - lo)), B(ps, 0, 3 * (hi - lo)))
+
+        def turn(lo, hi):
+            vtrans(B("tr", lo, hi), B("z1", 3 * lo + 2, 3 * hi, 3))
 
         def best2(lo, hi):
-            vtrans(B("tr", lo, hi), B("z1", 3 * lo + 2, 3 * hi, 3))
             scan(B("s2", lo, hi), B("RS16", 0, hi - lo), B("tr", lo, hi))
 
-        gat(0)
-        gat(1)
-        gat(2)
-        for nm in ORDER[:5]:
-            sums(nm)
-        best1(0, 96, "psKA", 0)
-        best2(0, 96)
-        gat(3)
-        for nm in ORDER[5:]:
-            sums(nm)
-        best1(144, 256, "psKC", 0)
-        best1(96, 144, "psKB", 0)
-        best2(96, 256)
-        last = t == NR - 1
-        bi, acc = B("s2", 15, 256, 16), B("acc%d" % t, 0, 16)
-        ts(B("sc"), bi, 6, None, AL.logical_shift_right)
-        ts(B("z16"), bi, 48, None, AL.bitwise_and)
-        ts(B("st"), bi, 15, None, AL.bitwise_and)
-        tt(acc, B("sc"), B("thr"), AL.is_lt)
-        tt(B("SWa", 0, 16), B("z16"), acc, AL.mult)
-        tt(B("SWa", 16, 32), B("st"), acc, AL.mult)
-        swap(("SWa", 0), 0, "ilist", "E16")
-        swap(("SWa", 16), 16)
-        ts(B("e2"), B("z16"), 32.0, None, AL.is_ge)
-        ts(B("e3"), B("z16"), 48.0, None, AL.is_ge)
-        tt(B("t2"), B("e2"), B("dn1"), AL.mult)
-        tt(B("t3"), B("e3"), B("dn2"), AL.mult)
-        tt(B("b1"), n0, B("t2"), AL.add)
-        vcopy(B("offB"), B("psS", 0, 32))
-        agather(B("Rb"), B(w, 32, 1056), B("offB", 0, 16))
-        vgather(B("OH"), B("ZI"), B("offB", 16, 32))
-        mm(B("psD", 0, 256), B("BLK"), ro(0, 256), True, False)
-        mm(B("psD", 0, 256), B("NBLK"), B("Rb"), False, True)
-        mm(B("psD", 256, 512), B("I"), B("Rb"), True, True)
-        tt(B("bn"), B("b1"), B("t3"), AL.add)
+        def accept(lo, hi):
+            a, b = lo // 16, hi // 16
+            bi, ac = B("s2", lo + 15, hi, 16), B("IND", a, b)
+            ts(B("st", a, b), bi, 15, None, AL.bitwise_and)
+            ts(B("z16", a, b), bi, 48, None, AL.bitwise_and)
+            tt(ac, bi, B("thr", a, b), AL.is_lt)
+            vcopy(B("SWa", 16 + a, 16 + b), B("st", a, b))
+            tt(B("SWa", a, b), B("z16", a, b), ac, AL.mult)
+            swap(("SWa", 16), 16, None, "E", a, b)
+            swap(("SWa", 0), 0, "ilist", "E16", a, b)
+
+        def offsets(lo, hi):
+            a, b = lo // 16, hi // 16
+            vcopy(B("offB", a, b), B("psS", a, b))
+            vcopy(B("offB", 16 + a, 16 + b), B("psS", 16 + a, 16 + b))
+            vgather(B("OH", lo, hi), B("ZI"), B("offB", 16 + a, 16 + b))
+
+        def newlist(lo, hi, ps):
+            agather(B("Rb", lo, hi), B(w, 16, 1040), B("offB", lo // 16, hi // 16))
+            mm(B(ps, 0, hi - lo), B("BLK"), ro(lo, hi), True, False)
+            mm(B(ps, 0, hi - lo), B("NBLK"), B("Rb", lo, hi), False, True)
+            mm(B(ps, 256, 256 + hi - lo), B("I"), B("Rb", lo, hi), True, True)
+
+        def putlist(lo, hi, ps):
+            tt(B("md", lo, hi), B(ps, 0, hi - lo), B("OH", lo, hi), AL.mult)
+            out = B("Rf", lo, hi) if last else B(wn, 16 + lo, 16 + hi)
+            tt(out, B(ps, 256, 256 + hi - lo), B("md", lo, hi), AL.add)
+            if last:
+                store("s", T.yr[:, lo:hi], out, "st%d" % (3 if lo else 0))
+
+        for s0, s1 in ABLK + [ALATE]:
+            absd(s0, s1)
+        for blk in DBLK:
+            gat(blk)
+        for nm in ORDER:
+            sums(nm[0], (ABLK if nm[0] == "A" else DBLK)[int(nm[1])])
+        vcopy(B("B1", 0, 256, 16), B("psS", 32, 48))
+        vtrans(B("X"), B("B1"))
+        gat(DLATE)
+        sums("D", DLATE)
+        sums("A", ALATE)
+        best1(32, DE, "psKC")
+        best1(DE, V, "psKA")
+        turn(32, V)
+        best2(32, V)
+        accept(32, V)
+        agather(B("nX", 0, 256), B("X"), B("n0U"))
+        agather(B("X2"), B("X"), B("srcU"))
+        agather(B("nX", 256, 512), B("X2"), B("n0U"))
+        best1(0, 32, "psKB")
+        vtrans(B("T12", 0, 256), B("nX", 0, 256))
+        turn(0, 32)
+        offsets(32, V)
+        best2(0, 32)
+        newlist(32, V, "psD")
+        vtrans(B("T12", 256, 512), B("nX", 256, 512))
+        accept(0, 32)
+        n1, n2 = B("T12", 0, 256, 16), B("T12", 256, 512, 16)
+        acc = B("IND", 0, 16)
+        tt(B("PQ", 16, 32), n1, n0, AL.subtract)
+        tt(B("PQ", 32, 48), n2, n1, AL.subtract)
+        ts(B("IND", 16, 32), B("SWa", 0, 16), 32.0, None, AL.is_ge)
+        ts(B("IND", 32, 48), B("SWa", 0, 16), 48.0, None, AL.is_ge)
+        offsets(0, 32)
+        newlist(0, 32, "psP1")
+        tt(B("TP"), B("IND"), B("PQ"), AL.mult)
+        putlist(32, V, "psD")
         if not last:
-            wn = W[t + 1]
-            own = B(w, 16, 32)
-            tt(B("d1"), B("bn"), own, AL.subtract)
-            tt(B("d2"), B("d1"), acc, AL.mult)
-            tt(B(wn, 16, 32), B("d2"), own, AL.add)
-            swap((wn, 16), 32)
-        tt(B("md"), B("psD", 0, 256), B("OH"), AL.mult)
-        if not last:
-            tt(B(wn, 32, 288), B("psD", 256, 512), B("md"), AL.add)
-            vcopy(B(wn, 0, 16), B("psS", 32, 48))
-            send(t + 1)
+            for h in range(2):
+                o = B("psP0", h, 16, 2)
+                mm(o, B("I"), B(w, h, 16, 2), True, False)
+                for f in range(3):
+                    for e in range(2):
+                        k = 128 * (2 * e + h)
+                        mm(o, B("E", k, k + 128), B("TP", 16 * f + e, 16 * f + 16, 2), False, f == 2 and e == 1)
         else:
-            tt(B("Rf"), B("psD", 256, 512), B("md"), AL.add)
-            op("s", lambda e: e.dma_start(T.yr[:], T.Rf[:]), [B("Rf")], [], sem="st0", inc=16)
-        ts(B("h1"), B("bn"), 13.0, None, AL.mult)
-        tt(B("h2"), B("h1"), B("sc"), AL.add)
-        ts(B("h3"), B("h2"), 255, None, AL.bitwise_and)
-        tt(B("d3"), B("h3"), n2, AL.subtract)
-        tt(B("d4"), B("d3"), acc, AL.mult)
-        tt(B("d5"), B("sc"), B("F"), AL.subtract)
-        tt(B("d6"), B("d5"), acc, AL.mult)
+            ts(B("sc"), B("s2", 15, 256, 16), 6, None, AL.logical_shift_right)
+        tt(B("b1"), B("TP", 0, 16), B("TP", 16, 32), AL.add)
         if not last:
-            nn = "nL" if nown[0] == "nLn" else "nLn"
-            tt(B(nn), B("d4"), n2, AL.add)
-            swap((nn, 0), 48)
-            nown[0] = nn
+            vcopy(B(wn, 0, 16), B("psP0", 0, 16))
+            putlist(0, 32, "psP1")
+            send(t + 1, pieces(t + 1)[0])
+        tt(B("bn"), B("TP", 32, 48), B("b1"), AL.add)
+        tt(B(sown[1]), B("bn"), srcl, AL.add)
+        ts(B("h1"), B(sown[1]), 13.0, None, AL.mult)
+        if last:
+            putlist(0, 32, "psP1")
+        else:
+            ts(B("sc"), B("s2", 15, 256, 16), 6, None, AL.logical_shift_right)
+        tt(B("h2"), B("h1"), B("sc"), AL.add)
+        tt(B("d5"), B("sc"), B("F"), AL.subtract)
+        ts(B("h3"), B("h2"), 255, None, AL.bitwise_and)
+        tt(B("d6"), B("d5"), acc, AL.mult)
+        tt(B("d3"), B("h3"), n2, AL.subtract)
+        if not last:
             tt(B("F"), B("d6"), B("F"), AL.add)
-            vcopy(B("n0U"), B("psS", 48, 64))
+            tt(B("d4"), B("d3"), acc, AL.mult)
+            tt(B(nown[1]), B("d4"), n2, AL.add)
+            swap((nown[1], 0), 48)
+            vcopy(B("acc%d" % t, 0, 16), acc)
             vcopy(B("acc%d" % t, 16, 32), acc)
+            vcopy(B("n0U"), B("psS", 48, 64))
             k = 0
             for r in range(t + 1):
                 for s in range(8):
@@ -525,9 +574,11 @@ def rank_program(g, core, T, topo):
             vcopy(B("Ai"), B("psS", 64, 80))
             ts(B("A7"), B("Ai"), 7, None, AL.bitwise_and)
             tt(B("thr"), B("F"), B("A7"), AL.subtract)
+            ts(B("thr"), B("thr"), 64.0, None, AL.mult)
+            nown, sown = nown[::-1], sown[::-1]
         else:
-            memset(B("B2"), 0.0)
             tt(B("B2", 0, 256, 16), B("d6"), B("F"), AL.add)
+            tt(B("d4"), B("d3"), acc, AL.mult)
             tt(B("B2", 1, 256, 16), B("d4"), n2, AL.add)
             vtrans(B("oT"), B("B2"))
             op("s", lambda e: e.dma_start(T.yf[:], T.oT[0:128:16, :]), [B("oT")], [], sem="st1", inc=16)

@@ -6,7 +6,7 @@ AL = AluOpType
 AF = ActivationFunctionType
 NR = 3
 V = 256
-DS, DE = 16, 130
+DS, DE = 16, 128
 NA, ND = DS + V - DE, DE - DS
 ABLK = [(DE + (V - DE) * i // 4, DE + (V - DE) * (i + 1) // 4) for i in range(4)]
 ALATE = (0, DS)
@@ -370,23 +370,25 @@ def rank_program(g, core, T, topo):
 
         lists = B(land, 16, PAY)
         f0 = 2 * (DE // 32)
-        rest = [(0, f0), (f0 + 4, 16)]
+        f1 = f0 + 2 * ((DE + 15) // 32 - DE // 32 + 1)
+        rest = [(0, f0), (f1, 16)]
 
         def nx(c0, c1):
             return B("n0U", c0, c1)
         vcopy(B("srcU"), B(land, 0, 16))
         agather(B("LQ1", 0, 128), lists, B("srcU", 0, 8))
         vgather(B("LQ1", 128, 256), lists, B("srcU", 8, 16))
-        vgather(rc(0, 16 * f0, 16 * f0 + 64), lists, nx(f0, f0 + 4))
+        vgather(rc(0, 16 * f0, 16 * f1), lists, nx(f0, f1))
         agather(B("LQ2", 0, 128), B("LQ1"), B("srcU", 0, 8))
         vgather(B("LQ2", 128, 256), B("LQ1"), B("srcU", 8, 16))
-        vgather(rc(1, 16 * f0, 16 * f0 + 64), B("LQ1"), nx(f0, f0 + 4))
-        vgather(rc(2, 16 * f0, 16 * f0 + 64), B("LQ2"), nx(f0, f0 + 4))
+        vgather(rc(1, 16 * f0, 16 * f1), B("LQ1"), nx(f0, f1))
+        vgather(rc(2, 16 * f0, 16 * f1), B("LQ2"), nx(f0, f1))
         for c0, c1 in rest:
             agather(rc(1, 16 * c0, 16 * c1), B("LQ1"), nx(c0, c1))
             agather(rc(2, 16 * c0, 16 * c1), B("LQ2"), nx(c0, c1))
-        for ci, ch in enumerate(CHUNKS):
-            c0, c1 = ch[0][1], ch[-1][2]
+        def prefix(ci):
+            ch = CHUNKS[ci]
+            c0 = ch[0][1]
             P = "psP%d" % (ci % 2)
             for kind, s0, s1 in ch:
                 n = s1 - s0
@@ -401,21 +403,52 @@ def rank_program(g, core, T, topo):
                     mm(oh, B("I"), B("c4096", 0, n), True, False)
                     mm(oh, B("BLK"), ro(s0, s1), False, False)
                     mm(oh, B("TMO"), rc(z, s0, s1), False, True)
+
+        def times(ci):
+            c0, c1 = CHUNKS[ci][0][1], CHUNKS[ci][-1][2]
             n = 6 * (c1 - c0)
-            va, vb = ("v1a", "v2a") if ci % 2 == 0 else ("v1b", "v2b")
-            tt(B(va, 0, n), B(P, 0, n), B("odd", 6 * c0, 6 * c1), AL.mult)
-            ts(B(vb, 0, n), B(va, 0, n), 2, 4095, AL.arith_shift_right, AL.bitwise_and)
-            vcopy(B("off", 6 * c0, 6 * c1), B(vb, 0, n))
-            if ci == 0:
-                for a, b in rest:
-                    vgather(rc(0, 16 * a, 16 * b), lists, nx(a, b))
-        for P, c0, c1 in (("psQ", DE, V), ("psP0", 32, DE), ("psP1", 0, 32)):
+            tt(B("v1" + "ab"[ci % 2], 0, n), B("psP%d" % (ci % 2), 0, n), B("odd", 6 * c0, 6 * c1), AL.mult)
+
+        def floor(ci):
+            n = 6 * (CHUNKS[ci][-1][2] - CHUNKS[ci][0][1])
+            ts(B("v2" + "ab"[ci % 2], 0, n), B("v1" + "ab"[ci % 2], 0, n), 2, 4095, AL.arith_shift_right, AL.bitwise_and)
+
+        def place(ci):
+            c0, c1 = CHUNKS[ci][0][1], CHUNKS[ci][-1][2]
+            vcopy(B("off", 6 * c0, 6 * c1), B("v2" + "ab"[ci % 2], 0, 6 * (c1 - c0)))
+
+        def allowed(P, c0, c1):
             for z in range(3):
                 o = B(P, z, 3 * (c1 - c0), 3)
                 mm(o, B("I"), B("cm127", 0, c1 - c0), True, False)
                 mm(o, B("BLK"), ro(c0, c1), False, False)
                 mm(o, B("IMO"), rc(z, c0, c1), False, True)
             ts(B("pen", 3 * c0, 3 * c1), B(P, 0, 3 * (c1 - c0)), MAGIC, MAGIC, AL.add, AL.not_equal)
+
+        prefix(0)
+        a, b = rest[0]
+        vgather(rc(0, 16 * a, 16 * b), lists, nx(a, b))
+        times(0)
+        floor(0)
+        place(0)
+        a, b = rest[1]
+        vgather(rc(0, 16 * a, 16 * b), lists, nx(a, b))
+        for c in (1, 3):
+            prefix(c)
+            prefix(c + 1)
+            times(c)
+            times(c + 1)
+            floor(c)
+            floor(c + 1)
+            place(c)
+            place(c + 1)
+        prefix(5)
+        times(5)
+        allowed("psQ", DE, V)
+        floor(5)
+        allowed("psP0", 32, DE)
+        place(5)
+        allowed("psP1", 0, 32)
         swap((land, 0), 32)
         n0, srcl = B(nown[0]), B(sown[0])
         tt(B("PQ", 0, 16), n0, srcl, AL.subtract)
@@ -434,7 +467,9 @@ def rank_program(g, core, T, topo):
                 c = 6 * s0 + gh * 3 * (s1 - s0)
                 of, x, o = B("off", c, c + 3 * (s1 - s0)), B("Xe", 48 * (s0 - DS), 48 * (s1 - DS)), B("dd", lo, lo + n)
                 op("v", lambda e: e.tensor_tensor(o[0], ind(B("S"), of), x[0], AL.subtract), [B("S"), of, x], [o])
-                ts(B("rr", lo, lo + n), o, 0.0, -2.0, AL.min, AL.mult)
+            for gh in range(2):
+                lo = base + gh * n
+                ts(B("rr", lo, lo + n), B("dd", lo, lo + n), 0.0, -2.0, AL.min, AL.mult)
 
         def sums(kind, blk):
             s0, s1 = blk
@@ -479,16 +514,19 @@ def rank_program(g, core, T, topo):
             a, b = lo // 16, hi // 16
             vcopy(B("offB", a, b), B("psS", a, b))
             vcopy(B("offB", 16 + a, 16 + b), B("psS", 16 + a, 16 + b))
-            vgather(B("OH", lo, hi), B("ZI"), B("offB", 16 + a, 16 + b))
+
+        def readlist(lo, hi):
+            agather(B("Rb", lo, hi), B(w, 16, 1040), B("offB", lo // 16, hi // 16))
 
         def newlist(lo, hi, ps):
-            agather(B("Rb", lo, hi), B(w, 16, 1040), B("offB", lo // 16, hi // 16))
             mm(B(ps, 0, hi - lo), B("BLK"), ro(lo, hi), True, False)
             mm(B(ps, 0, hi - lo), B("NBLK"), B("Rb", lo, hi), False, True)
             mm(B(ps, 256, 256 + hi - lo), B("I"), B("Rb", lo, hi), True, True)
 
-        def putlist(lo, hi, ps):
+        def site(lo, hi, ps):
             tt(B("md", lo, hi), B(ps, 0, hi - lo), B("OH", lo, hi), AL.mult)
+
+        def putlist(lo, hi, ps):
             out = B("Rf", lo, hi) if last else B(wn, 16 + lo, 16 + hi)
             tt(out, B(ps, 256, 256 + hi - lo), B("md", lo, hi), AL.add)
             if last:
@@ -513,24 +551,30 @@ def rank_program(g, core, T, topo):
         agather(B("nX", 0, 256), B("X"), B("n0U"))
         agather(B("X2"), B("X"), B("srcU"))
         agather(B("nX", 256, 512), B("X2"), B("n0U"))
-        best1(0, 32, "psKB")
         vtrans(B("T12", 0, 256), B("nX", 0, 256))
-        turn(0, 32)
-        offsets(32, V)
-        best2(0, 32)
-        newlist(32, V, "psD")
-        vtrans(B("T12", 256, 512), B("nX", 256, 512))
-        accept(0, 32)
+        best1(0, 32, "psKB")
         n1, n2 = B("T12", 0, 256, 16), B("T12", 256, 512, 16)
         acc = B("IND", 0, 16)
         tt(B("PQ", 16, 32), n1, n0, AL.subtract)
-        tt(B("PQ", 32, 48), n2, n1, AL.subtract)
+        turn(0, 32)
+        offsets(32, V)
+        best2(0, 32)
+        readlist(32, V)
+        agather(B("OH", 32, V), B("ZI"), B("offB", 18, 32))
+        accept(0, 32)
+        newlist(32, V, "psD")
+        vtrans(B("T12", 256, 512), B("nX", 256, 512))
         ts(B("IND", 16, 32), B("SWa", 0, 16), 32.0, None, AL.is_ge)
         ts(B("IND", 32, 48), B("SWa", 0, 16), 48.0, None, AL.is_ge)
+        tt(B("PQ", 32, 48), n2, n1, AL.subtract)
         offsets(0, 32)
+        readlist(0, 32)
+        agather(B("OH", 0, 32), B("ZI"), B("offB", 16, 18))
         newlist(0, 32, "psP1")
         tt(B("TP"), B("IND"), B("PQ"), AL.mult)
-        putlist(32, V, "psD")
+        if last:
+            tt(B("b1"), B("TP", 0, 16), B("TP", 16, 32), AL.add)
+        site(32, V, "psD")
         if not last:
             for h in range(2):
                 o = B("psP0", h, 16, 2)
@@ -539,24 +583,27 @@ def rank_program(g, core, T, topo):
                     for e in range(2):
                         k = 128 * (2 * e + h)
                         mm(o, B("E", k, k + 128), B("TP", 16 * f + e, 16 * f + 16, 2), False, f == 2 and e == 1)
-        else:
-            ts(B("sc"), B("s2", 15, 256, 16), 6, None, AL.logical_shift_right)
-        tt(B("b1"), B("TP", 0, 16), B("TP", 16, 32), AL.add)
         if not last:
+            site(0, 32, "psP1")
+            putlist(32, V, "psD")
             vcopy(B(wn, 0, 16), B("psP0", 0, 16))
             putlist(0, 32, "psP1")
             send(t + 1, pieces(t + 1)[0])
+            tt(B("b1"), B("TP", 0, 16), B("TP", 16, 32), AL.add)
         tt(B("bn"), B("TP", 32, 48), B("b1"), AL.add)
+        ts(B("sc"), B("s2", 15, 256, 16), 6, None, AL.logical_shift_right)
+        if last:
+            site(0, 32, "psP1")
         tt(B(sown[1]), B("bn"), srcl, AL.add)
+        if last:
+            putlist(32, V, "psD")
+        tt(B("d5"), B("sc"), B("F"), AL.subtract)
         ts(B("h1"), B(sown[1]), 13.0, None, AL.mult)
         if last:
             putlist(0, 32, "psP1")
-        else:
-            ts(B("sc"), B("s2", 15, 256, 16), 6, None, AL.logical_shift_right)
-        tt(B("h2"), B("h1"), B("sc"), AL.add)
-        tt(B("d5"), B("sc"), B("F"), AL.subtract)
-        ts(B("h3"), B("h2"), 255, None, AL.bitwise_and)
         tt(B("d6"), B("d5"), acc, AL.mult)
+        tt(B("h2"), B("h1"), B("sc"), AL.add)
+        ts(B("h3"), B("h2"), 255, None, AL.bitwise_and)
         tt(B("d3"), B("h3"), n2, AL.subtract)
         if not last:
             tt(B("F"), B("d6"), B("F"), AL.add)

import numpy as np
from concourse.bass import DstId, RemoteDMATransfer
from concourse.mybir import dt, AluOpType, AxisListType, ActivationFunctionType

AL = AluOpType
AF = ActivationFunctionType
NR = 3
V = 256
DS, DE = 16, 128
NA, ND = DS + V - DE, DE - DS
ABLK = [(DE + (V - DE) * i // 4, DE + (V - DE) * (i + 1) // 4) for i in range(4)]
ALATE = (0, DS)
DBLK = [(32, 64), (64, 96), (96, DE)]
DLATE = (DS, 32)
CHUNKS = [[("A", DE, DE + 16)], [("A", DE + 16, DE + 80)], [("A", DE + 80, V)],
          [("D", 32, 64), ("D", 64, 96)], [("D", 96, DE)], [("A", 0, DS), ("D", DS, 32)]]
ORDER = ["A0", "D0", "A1", "D1", "A2", "D2", "A3"]
KEYBANK = [(0, 32, "psKB"), (32, DE, "psKC"), (DE, V, "psKA")]
PAY = 272
CUT = 1024
BIG = 33554432.0
MAGIC = 1.5 * 2.0 ** 31


def sb(cols, kind="bfloat16"):
    return ("sbuf", [128, cols], kind)


SCRATCH = {
    "S": sb(4096), "obs_s": sb(256), "nobs": sb(256, "float32"), "Xe": sb(ND * 48),
    "rawR": sb(256, "int32"), "raws": sb(16, "int32"), "rawn": sb(16, "int32"),
    "fitb": sb(256, "int32"), "fitf": sb(256, "float32"), "fitt": sb(256, "float32"),
    "W0": sb(1040), "W1": sb(1040), "W2": sb(1040), "land0": sb(PAY), "land1": sb(PAY), "land2": sb(PAY),
    "LQ1": sb(256), "LQ2": sb(256), "srcU": sb(16, "uint16"), "n0U": sb(16, "uint16"), "offB": sb(32, "uint16"),
    "B1": sb(256), "X": sb(256), "X2": sb(256), "nX": sb(512), "T12": sb(512),
    "off": sb(1536, "uint16"), "odd": sb(1536, "float32"),
    "v1a": sb(384, "int32"), "v1b": sb(384, "int32"), "v2a": sb(384, "int32"), "v2b": sb(384, "int32"),
    "pen": sb(768), "A": sb(NA * 96), "dd": sb(ND * 96), "rr": sb(ND * 96),
    "z1": sb(768, "float32"), "tr": sb(256, "float32"), "s2": sb(256, "int32"),
    "sc": sb(16, "int32"), "z16": sb(16, "int32"), "st": sb(16, "int32"), "SWa": sb(32),
    "acc0": sb(32), "acc1": sb(32), "IND": sb(48), "PQ": sb(48), "TP": sb(48),
    "nL": sb(16), "nLn": sb(16), "srcA": sb(16), "srcB": sb(16),
    "F": sb(16, "float32"), "thr": sb(16, "float32"), "Ai": sb(16, "int32"), "A7": sb(16, "int32"),
    "b1": sb(16, "float32"), "bn": sb(16, "float32"), "h1": sb(16, "float32"), "h2": sb(16, "int32"), "h3": sb(16, "int32"),
    "d3": sb(16, "float32"), "d4": sb(16, "float32"), "d5": sb(16, "float32"), "d6": sb(16, "float32"),
    "Rb": sb(256), "OH": sb(256), "md": sb(256), "Rf": sb(256, "float32"), "B2": sb(256, "float32"), "oT": sb(256, "float32"),
    "ones": sb(128), "I": sb(128), "BLK": sb(128), "TRI": sb(128), "TMO": sb(128), "IMO": sb(128), "NBLK": sb(128), "BIGI": sb(128),
    "BLK32": sb(128), "B48": ("sbuf", [128, 8, 48], "bfloat16"), "WT": ("sbuf", [128, 248, 16], "bfloat16"), "E": sb(512), "E16": sb(512),
    "c4096": sb(64), "cm127": sb(160), "pi": sb(1, "int32"), "pj": sb(1, "int32"), "jcol": sb(1, "float32"),
    "kct": sb(120, "float32"), "KC": sb(120), "ilt": sb(16, "float32"), "ilist": sb(16), "zit": sb(16, "float32"), "ZI": sb(16),
    "RS3": sb(420, "float32"), "RS16": sb(256, "float32"),
    "psP0": ("psum", [128, 512], "float32"), "psP1": ("psum", [128, 512], "float32"), "psQ": ("psum", [128, 512], "float32"),
    "psKA": ("psum", [128, 512], "float32"), "psKB": ("psum", [128, 512], "float32"), "psKC": ("psum", [128, 512], "float32"),
    "psS": ("psum", [128, 512], "float32"), "psD": ("psum", [128, 512], "float32"),
}
SEMAPHORES = (["qv", "qa", "qp", "qg", "go", "ldf"] + ["ld%d" % i for i in range(6)] + ["st%d" % i for i in range(4)]
              + ["%s%s%d" % (n, p, t) for n in ("arr", "hop", "loc", "hl") for t in range(NR) for p in "EL"])


def route(q, t, cores, topo):
    n = len(cores)
    src, dst = cores[q], cores[(q - 1 - (t % (n - 1))) % n]
    if topo.may_write(src, dst):
        return dst, None
    for c in topo.cores_of(src):
        if c not in cores and topo.die(c) == topo.die(src) and topo.may_write(c, dst):
            return dst, c
    return dst, None


def pick(src, dst, topo):
    e = topo.engines(src, dst)[:8]
    return sum(1 << i for i in e), len(e)


def pieces(t):
    return [("L", 0, 16), ("E", 16, PAY)] if t == 0 else [("E", 0, PAY)]


def relay_program(g, core, T, topo):
    held = []
    for t in range(NR):
        for q in range(len(T.cores)):
            dst, via = route(q, t, T.cores, topo)
            if via != core:
                continue
            _, n1 = pick(T.cores[q], core, topo)
            m, n2 = pick(core, dst, topo)
            rid, pid = topo.addr(dst, core)
            for p, a, b in pieces(t):
                land = T["land%d" % t][:, a:b]
                g.wait_ge(T.sem["hop%s%d" % (p, t)], n1)
                g.remote_dma(out_ap=land, in_ap=land, remote_sem=T.sem["arr%s%d" % (p, t)], local_sem=T.sem["hl%s%d" % (p, t)],
                             pid=pid, routing_id=rid, dma_engine_mask=m)
                held.append(("hl%s%d" % (p, t), n2))
    for s, n in held:
        g.wait_ge(T.sem[s], n)


def rank_program(g, core, T, topo):
    rank = T.rank_of(core)
    if rank is None:
        relay_program(g, core, T, topo)
        return
    ENG = {"v": g.vector, "a": g.scalar, "p": g.tensor, "g": g, "s": g.sync}
    total, known, hist, rec, bank = {}, {k: {} for k in ENG}, {}, {}, {}
    nload = [0]

    def need(want, tok):
        s, c = tok
        if want.get(s, 0) < c:
            want[s] = c

    def learn(q, s, c):
        k = known[q]
        for a, b in hist.get((s, c), {}).items():
            if k.get(a, 0) < b:
                k[a] = b
        if k.get(s, 0) < c:
            k[s] = c

    def wait(q, want):
        for s, c in sorted(want.items(), key=lambda x: x[0]):
            if known[q].get(s, 0) < c:
                ENG[q].wait_ge(T.sem[s], c)
                learn(q, s, c)

    def step(v):
        return v[4] if len(v) > 4 else 1

    def clash(r, v):
        s = step(v)
        return r[1] < v[3] and v[2] < r[2] and not (s > 1 and s == r[5] and (r[1] - v[2]) % s)

    def covers(v, r):
        s = step(v)
        return v[2] <= r[1] and r[2] <= v[3] and (s == 1 or (s == r[5] and (r[1] - v[2]) % s == 0))

    def op(q, fn, reads, writes, sem=None, inc=1, then=True):
        own = sem is None
        s = "q" + q if own else sem
        tag = q if own else "x" + sem
        want = {}
        for v in reads + writes:
            if v[1][:2] == "ps":
                for a, tok in bank.get(v[1], {}).items():
                    if a != tag:
                        need(want, tok)
        for v in reads:
            for r in rec.get(v[1], []):
                if r[0] == "w" and clash(r, v):
                    need(want, r[4])
        for v in writes:
            for r in rec.get(v[1], []):
                if (r[3] != tag or r[0] == "w") and clash(r, v):
                    need(want, r[4])
        wait(q, want)
        ins = fn(ENG[q])
        total[s] = total.get(s, 0) + inc
        tok = (s, total[s])
        if then:
            ins.then_inc(T.sem[s], inc)
        hist[tok] = dict(known[q])
        for v in reads:
            if v[1][:2] == "ps":
                bank.setdefault(v[1], {})[tag] = tok
                continue
            L = [r for r in rec.get(v[1], []) if not (r[0] == "r" and r[3] == tag and covers(v, r))]
            L.append(("r", v[2], v[3], tag, tok, step(v)))
            rec[v[1]] = L
        for v in writes:
            if v[1][:2] == "ps":
                bank.setdefault(v[1], {})[tag] = tok
                continue
            L = [r for r in rec.get(v[1], []) if not covers(v, r)]
            L.append(("w", v[2], v[3], tag, tok, step(v)))
            rec[v[1]] = L
        return tok

    def arrived(name, lo, hi, sem, n):
        total[sem] = total.get(sem, 0) + n
        rec.setdefault(name, []).append(("w", lo, hi, "x" + sem, (sem, total[sem]), 1))

    def B(name, lo=0, hi=None, step=1):
        t = T[name]
        hi = t.shape[1] if hi is None else hi
        return (t[:, lo:hi] if step == 1 else t[:, lo:hi:step], name, lo, hi, step)

    def ind(win, of):
        return win[0].indirect(of[0])

    def tt(out, a, b, o):
        return op("v", lambda e: e.tensor_tensor(out[0], a[0], b[0], o), [a, b], [out])

    def ts(out, a, s1, s2, o0, o1=None, col=None):
        x = col[0] if col else s1
        if o1 is None:
            return op("v", lambda e: e.tensor_scalar(out[0], a[0], x, None, o0), [a] + ([col] if col else []), [out])
        return op("v", lambda e: e.tensor_scalar(out[0], a[0], x, s2, o0, o1), [a] + ([col] if col else []), [out])

    def vcopy(out, a):
        return op("v", lambda e: e.tensor_copy(out[0], a[0]), [a], [out])

    def acopy(out, a):
        return op("a", lambda e: e.activation(out[0], a[0], AF.Copy), [a], [out])

    def vgather(out, win, of):
        return op("v", lambda e: e.tensor_copy(out[0], ind(win, of)), [win, of], [out])

    def agather(out, win, of):
        return op("a", lambda e: e.activation(out[0], ind(win, of), AF.Copy), [win, of], [out])

    def vtrans(out, a):
        return op("v", lambda e: e.transpose(out[0], a[0]), [a], [out])

    def memset(out, c):
        return op("v", lambda e: e.memset(out[0], c), [], [out])

    def scan(out, d0, d1):
        return op("v", lambda e: e.tensor_tensor_scan(out[0], d0[0], d1[0], 0.0, AL.add, AL.min), [d0, d1], [out])

    def mm(out, l, r, start, stop):
        return op("p", lambda e: e.matmul(out[0], l[0], r[0], start, stop), [l, r], [out])

    def load(q, out, src):
        k = nload[0]
        nload[0] += 1
        return op(q, lambda e: e.dma_start(out[0], src), [], [out], sem="ld%d" % k, inc=16)

    def store(q, out, src, sem):
        return op(q, lambda e: e.dma_start(out, src[0]), [src], [], sem=sem, inc=16)

    def iota(out, pattern, base, cm, f=True):
        if f:
            return op("g", lambda e: e.iota(out[0], pattern, base, cm, allow_small_or_imprecise_dtypes=True), [], [out])
        return op("g", lambda e: e.iota(out[0], pattern, base, cm), [], [out])

    def sel(out, a, pattern, cmp, base, cm):
        return op("g", lambda e: e.affine_select(out[0], a[0], pattern, cmp, 0.0, base, cm), [a], [out])

    def apos(s):
        return s if s < DS else s - ND

    def weight(gh, k):
        n = 15 * gh + k
        return (T.WT[:, 8 * n:8 * n + 8, :], "WT", n, n + 1)

    def put_weight(gh, k, q):
        lo = 15 - k if gh == 0 else 31 - k
        (vcopy if q == "v" else acopy)(weight(gh, k), (T.B48[:, :, lo:lo + 16], "B48", 0, 384))

    def swap(field, col, extra=None, name="E", a=0, b=16):
        fb, fo = field
        for h in range(2):
            o = B("psS", col + a + h, col + b, 2)
            if extra is not None:
                mm(o, B("I"), B(extra, a + h, b, 2), True, False)
            for e in range(2):
                k = 128 * (2 * e + h)
                mm(o, B(name, k, k + 128), B(fb, fo + a + e, fo + b, 2), extra is None and e == 0, e == 1)

    W = ["W0", "W1", "W2"]
    load("s", B("rawR"), T.resid[:])
    load("a", B("raws"), T.src0[:])
    load("a", B("rawn"), T.nx0[:])
    load("s", B("S", 0, CUT), T.prof[:, 0:CUT])
    load("a", B("obs_s"), T.obs[:])
    memset(B("ones"), 1.0)
    memset(B("E"), 0.0)
    memset(B("fitb"), 0)
    op("v", lambda e: e.memset(T.B48[:, :, 0:16], 0.0), [], [("", "B48", 0, 384)])
    op("v", lambda e: e.memset(T.B48[:, :, 16:32], 64.0), [], [("", "B48", 0, 384)])
    op("v", lambda e: e.memset(T.B48[:, :, 32:48], 0.0), [], [("", "B48", 0, 384)])
    op("a", lambda e: e.dma_start(T.fitb[0:128:16, :], T.fit0[:]), [], [B("fitb")], sem="ldf", inc=16)
    iota(B("pi"), [[0, 1]], 0, 1, False)
    sel(B("I"), B("ones"), [[-1, 128]], AL.is_equal, 0, 1)
    iota(B("ilt"), [[16, 16]], 0, 0)
    iota(B("zit"), [[1, 16]], 0, 0)
    sel(B("BLK"), B("ones"), [[-16, 8], [0, 16]], AL.is_ge, 0, 1)
    sel(B("BLK"), B("BLK"), [[16, 8], [0, 16]], AL.is_ge, 15, -1)
    memset(B("RS3"), 0.0)
    memset(B("RS3", 0, 420, 3), BIG)
    vcopy(B("W0", 0, 16), B("raws"))
    vcopy(B("W0", 16, PAY), B("rawR"))

    def send(t, piece):
        p, a, b = piece
        dst, via = route(rank, t, T.cores, topo)
        to = dst if via is None else via
        m, n = pick(core, to, topo)
        rid, pid = topo.addr(to, core)
        rs, ls = T.sem["%s%s%d" % ("arr" if via is None else "hop", p, t)], "loc%s%d" % (p, t)
        src = B(W[t], a, b)
        op("g", lambda e: e.remote_dma(out_ap=T["land%d" % t][:, a:b], in_ap=src[0], remote_sem=rs, local_sem=T.sem[ls],
                                       pid=pid, routing_id=rid, dma_engine_mask=m), [src], [], sem=ls, inc=n, then=False)

    def expect(t):
        for q in range(len(T.cores)):
            dst, via = route(q, t, T.cores, topo)
            if dst == core:
                for p, a, b in pieces(t):
                    arrived("land%d" % t, a, b, "arr%s%d" % (p, t), pick(T.cores[q] if via is None else via, core, topo)[1])

    for piece in pieces(0):
        send(0, piece)
    g.sem_inc(T.sem["go"], 1)
    total["go"] = 1
    g.sync.wait_ge(T.sem["go"], 1)
    load("s", B("S", CUT, 4096), T.prof[:, CUT:4096])
    sel(B("TRI"), B("BLK"), [[1, 128]], AL.is_ge, 0, -1)
    iota(B("kct"), [[0, 40], [16, 3]], 16, 0)
    b48 = (T.B48[:], "B48", 0, 384)
    sel(b48, b48, [[-16, 8], [0, 48]], AL.is_ge, 0, 1)
    sel(b48, b48, [[16, 8], [0, 48]], AL.is_ge, 15, -1)
    iota(B("odd", 6 * DE, 1536), [[2, V - DE], [0, 6]], 2 * DE + 1, 0)
    iota(B("odd", 0, 6 * DS), [[2, DS], [0, 6]], 1, 0)
    for s0, s1 in DBLK + [DLATE]:
        iota(B("odd", 6 * s0, 6 * s1), [[0, 2], [2, s1 - s0], [0, 3]], 2 * s0 + 1, 0)
    sel(B("BLK32"), B("ones"), [[-32, 4], [0, 32]], AL.is_ge, 0, 1)
    sel(B("BLK32"), B("BLK32"), [[32, 4], [0, 32]], AL.is_ge, 31, -1)
    for e in range(2):
        for h in range(2):
            for a in range(4):
                k = 128 * (2 * e + h) + 32 * a
                vcopy(B("E", k + 16 * e, k + 16 * e + 16), B("I", 32 * a + 16 * h, 32 * a + 16 * h + 16))
    ts(B("E16"), B("E"), 16.0, None, AL.mult)
    vcopy(B("nL"), B("rawn"))
    swap(("nL", 0), 32)
    swap(("W0", 0), 48)
    vcopy(B("n0U"), B("rawn"))
    vcopy(B("nLn"), B("psS", 32, 48))
    vcopy(B("srcA"), B("psS", 48, 64))
    ts(B("pj"), B("pi"), 15, None, AL.bitwise_and)
    vcopy(B("jcol"), B("pj"))
    ts(B("ilist"), B("ilt"), None, None, AL.add, col=B("jcol"))
    ts(B("ZI"), B("zit"), None, None, AL.is_equal, col=B("jcol"))
    memset(B("c4096"), 4096.0)
    memset(B("cm127"), -127.5)
    tt(B("TMO"), B("TRI"), B("BLK"), AL.subtract)
    tt(B("IMO"), B("I"), B("BLK"), AL.subtract)
    ts(B("NBLK"), B("BLK"), -1.0, None, AL.mult)
    ts(B("BIGI"), B("I"), 4194304.0, None, AL.mult)
    memset(B("B1"), 0.0)
    memset(B("B2"), 0.0)
    memset(B("RS16"), 0.0)
    memset(B("RS16", 0, 256, 16), BIG)
    ts(B("nobs"), B("obs_s"), -1.0, None, AL.mult)
    for k in range(48):
        (acopy if k % 2 else vcopy)(B("Xe", k, ND * 48, 48), B("obs_s", DS, DE))
    for gh in range(2):
        for k in range(15 + gh):
            put_weight(gh, k, "a" if k % 2 else "v")
    ts(B("KC"), B("kct"), None, None, AL.add, col=B("jcol"))
    vcopy(B("fitf"), B("fitb"))
    vtrans(B("fitt"), B("fitf"))
    vcopy(B("F"), B("fitt", 0, 256, 16))
    ts(B("thr"), B("F"), 64.0, None, AL.mult)

    nown, sown = ["nLn", "nL"], ["srcA", "srcB"]
    for t in range(NR):
        w, land, last = W[t], "land%d" % t, t == NR - 1
        wn = None if last else W[t + 1]
        expect(t)

        def ro(a, b):
            return B(w, 16 + a, 16 + b)

        def rc(z, a, b):
            return B(w, 16 + 256 * (z + 1) + a, 16 + 256 * (z + 1) + b)

        lists = B(land, 16, PAY)
        f0 = 2 * (DE // 32)
        f1 = f0 + 2 * ((DE + 15) // 32 - DE // 32 + 1)
        rest = [(0, f0), (f1, 16)]

        def nx(c0, c1):
            return B("n0U", c0, c1)
        vcopy(B("srcU"), B(land, 0, 16))
        agather(B("LQ1", 0, 128), lists, B("srcU", 0, 8))
        vgather(B("LQ1", 128, 256), lists, B("srcU", 8, 16))
        vgather(rc(0, 16 * f0, 16 * f1), lists, nx(f0, f1))
        agather(B("LQ2", 0, 128), B("LQ1"), B("srcU", 0, 8))
        vgather(B("LQ2", 128, 256), B("LQ1"), B("srcU", 8, 16))
        vgather(rc(1, 16 * f0, 16 * f1), B("LQ1"), nx(f0, f1))
        vgather(rc(2, 16 * f0, 16 * f1), B("LQ2"), nx(f0, f1))
        for c0, c1 in rest:
            agather(rc(1, 16 * c0, 16 * c1), B("LQ1"), nx(c0, c1))
            agather(rc(2, 16 * c0, 16 * c1), B("LQ2"), nx(c0, c1))
        def prefix(ci):
            ch = CHUNKS[ci]
            c0 = ch[0][1]
            P = "psP%d" % (ci % 2)
            for kind, s0, s1 in ch:
                n = s1 - s0
                for z in range(3):
                    b = 6 * (s0 - c0)
                    if kind == "A":
                        og, oh = B(P, b + 2 * z, b + 6 * n, 6), B(P, b + 2 * z + 1, b + 6 * n, 6)
                    else:
                        og, oh = B(P, b + z, b + 3 * n, 3), B(P, b + 3 * n + z, b + 6 * n, 3)
                    mm(og, B("I"), B("c4096", 0, n), True, False)
                    mm(og, B("TRI"), rc(z, s0, s1), False, True)
                    mm(oh, B("I"), B("c4096", 0, n), True, False)
                    mm(oh, B("BLK"), ro(s0, s1), False, False)
                    mm(oh, B("TMO"), rc(z, s0, s1), False, True)

        def times(ci):
            c0, c1 = CHUNKS[ci][0][1], CHUNKS[ci][-1][2]
            n = 6 * (c1 - c0)
            tt(B("v1" + "ab"[ci % 2], 0, n), B("psP%d" % (ci % 2), 0, n), B("odd", 6 * c0, 6 * c1), AL.mult)

        def floor(ci):
            n = 6 * (CHUNKS[ci][-1][2] - CHUNKS[ci][0][1])
            ts(B("v2" + "ab"[ci % 2], 0, n), B("v1" + "ab"[ci % 2], 0, n), 2, 4095, AL.arith_shift_right, AL.bitwise_and)

        def place(ci):
            c0, c1 = CHUNKS[ci][0][1], CHUNKS[ci][-1][2]
            vcopy(B("off", 6 * c0, 6 * c1), B("v2" + "ab"[ci % 2], 0, 6 * (c1 - c0)))

        def allowed(P, c0, c1):
            for z in range(3):
                o = B(P, z, 3 * (c1 - c0), 3)
                mm(o, B("I"), B("cm127", 0, c1 - c0), True, False)
                mm(o, B("BLK"), ro(c0, c1), False, False)
                mm(o, B("IMO"), rc(z, c0, c1), False, True)
            ts(B("pen", 3 * c0, 3 * c1), B(P, 0, 3 * (c1 - c0)), MAGIC, MAGIC, AL.add, AL.not_equal)

        prefix(0)
        a, b = rest[0]
        vgather(rc(0, 16 * a, 16 * b), lists, nx(a, b))
        times(0)
        floor(0)
        place(0)
        a, b = rest[1]
        vgather(rc(0, 16 * a, 16 * b), lists, nx(a, b))
        for c in (1, 3):
            prefix(c)
            prefix(c + 1)
            times(c)
            times(c + 1)
            floor(c)
            floor(c + 1)
            place(c)
            place(c + 1)
        prefix(5)
        times(5)
        allowed("psQ", DE, V)
        floor(5)
        allowed("psP0", 32, DE)
        place(5)
        allowed("psP1", 0, 32)
        swap((land, 0), 32)
        n0, srcl = B(nown[0]), B(sown[0])
        tt(B("PQ", 0, 16), n0, srcl, AL.subtract)

        def absd(s0, s1):
            for s in range(s0, s1):
                p = 96 * apos(s)
                o, of, bi = B("A", p, p + 96), B("off", 6 * s, 6 * s + 6), B("nobs", s, s + 1)
                op("a", lambda e: e.activation(o[0], ind(B("S"), of), AF.Abs, bias=bi[0]), [B("S"), of, bi], [o])

        def gat(blk):
            s0, s1 = blk
            n, base = 48 * (s1 - s0), 96 * (s0 - DS)
            for gh in range(2):
                lo = base + gh * n
                c = 6 * s0 + gh * 3 * (s1 - s0)
                of, x, o = B("off", c, c + 3 * (s1 - s0)), B("Xe", 48 * (s0 - DS), 48 * (s1 - DS)), B("dd", lo, lo + n)
                op("v", lambda e: e.tensor_tensor(o[0], ind(B("S"), of), x[0], AL.subtract), [B("S"), of, x], [o])
            for gh in range(2):
                lo = base + gh * n
                ts(B("rr", lo, lo + n), B("dd", lo, lo + n), 0.0, -2.0, AL.min, AL.mult)

        def sums(kind, blk):
            s0, s1 = blk
            kb = [x for x in KEYBANK if x[0] <= s0 and s1 <= x[1]][0]
            o, n = B(kb[2], 3 * (s0 - kb[0]), 3 * (s1 - kb[0])), 3 * (s1 - s0)
            mm(o, B("I"), B("KC", 0, n), True, False)
            mm(o, B("BIGI"), B("pen", 3 * s0, 3 * s1), False, False)
            todo = []
            for gh in range(2):
                for buf in ("A",) if kind == "A" else ("dd", "rr"):
                    for k in range(15 + gh):
                        if kind == "A":
                            p = 96 * apos(s0)
                            todo.append((weight(gh, k), B(buf, p + 16 * gh + k, p + 32 * n, 32)))
                        else:
                            lo = 96 * (s0 - DS) + gh * 16 * n
                            todo.append((weight(gh, k), B(buf, lo + k, lo + 16 * n, 16)))
            for i, (wt, r) in enumerate(todo):
                mm(o, wt, r, False, i == len(todo) - 1)

        def best1(lo, hi, ps):
            scan(B("z1", 3 * lo, 3 * hi), B("RS3", 0, 3 * (hi - lo)), B(ps, 0, 3 * (hi - lo)))

        def turn(lo, hi):
            vtrans(B("tr", lo, hi), B("z1", 3 * lo + 2, 3 * hi, 3))

        def best2(lo, hi):
            scan(B("s2", lo, hi), B("RS16", 0, hi - lo), B("tr", lo, hi))

        def accept(lo, hi):
            a, b = lo // 16, hi // 16
            bi, ac = B("s2", lo + 15, hi, 16), B("IND", a, b)
            ts(B("st", a, b), bi, 15, None, AL.bitwise_and)
            ts(B("z16", a, b), bi, 48, None, AL.bitwise_and)
            tt(ac, bi, B("thr", a, b), AL.is_lt)
            vcopy(B("SWa", 16 + a, 16 + b), B("st", a, b))
            tt(B("SWa", a, b), B("z16", a, b), ac, AL.mult)
            swap(("SWa", 16), 16, None, "E", a, b)
            swap(("SWa", 0), 0, "ilist", "E16", a, b)

        def offsets(lo, hi):
            a, b = lo // 16, hi // 16
            vcopy(B("offB", a, b), B("psS", a, b))
            vcopy(B("offB", 16 + a, 16 + b), B("psS", 16 + a, 16 + b))

        def readlist(lo, hi):
            agather(B("Rb", lo, hi), B(w, 16, 1040), B("offB", lo // 16, hi // 16))

        def newlist(lo, hi, ps):
            mm(B(ps, 0, hi - lo), B("BLK"), ro(lo, hi), True, False)
            mm(B(ps, 0, hi - lo), B("NBLK"), B("Rb", lo, hi), False, True)
            mm(B(ps, 256, 256 + hi - lo), B("I"), B("Rb", lo, hi), True, True)

        def site(lo, hi, ps):
            tt(B("md", lo, hi), B(ps, 0, hi - lo), B("OH", lo, hi), AL.mult)

        def putlist(lo, hi, ps):
            out = B("Rf", lo, hi) if last else B(wn, 16 + lo, 16 + hi)
            tt(out, B(ps, 256, 256 + hi - lo), B("md", lo, hi), AL.add)
            if last:
                store("s", T.yr[:, lo:hi], out, "st%d" % (3 if lo else 0))

        for s0, s1 in ABLK + [ALATE]:
            absd(s0, s1)
        for blk in DBLK:
            gat(blk)
        for nm in ORDER:
            sums(nm[0], (ABLK if nm[0] == "A" else DBLK)[int(nm[1])])
        vcopy(B("B1", 0, 256, 16), B("psS", 32, 48))
        vtrans(B("X"), B("B1"))
        gat(DLATE)
        sums("D", DLATE)
        sums("A", ALATE)
        best1(32, DE, "psKC")
        best1(DE, V, "psKA")
        turn(32, V)
        best2(32, V)
        accept(32, V)
        agather(B("nX", 0, 256), B("X"), B("n0U"))
        agather(B("X2"), B("X"), B("srcU"))
        agather(B("nX", 256, 512), B("X2"), B("n0U"))
        vtrans(B("T12", 0, 256), B("nX", 0, 256))
        best1(0, 32, "psKB")
        n1, n2 = B("T12", 0, 256, 16), B("T12", 256, 512, 16)
        acc = B("IND", 0, 16)
        tt(B("PQ", 16, 32), n1, n0, AL.subtract)
        turn(0, 32)
        offsets(32, V)
        best2(0, 32)
        readlist(32, V)
        agather(B("OH", 32, V), B("ZI"), B("offB", 18, 32))
        accept(0, 32)
        newlist(32, V, "psD")
        vtrans(B("T12", 256, 512), B("nX", 256, 512))
        ts(B("IND", 16, 32), B("SWa", 0, 16), 32.0, None, AL.is_ge)
        ts(B("IND", 32, 48), B("SWa", 0, 16), 48.0, None, AL.is_ge)
        tt(B("PQ", 32, 48), n2, n1, AL.subtract)
        offsets(0, 32)
        readlist(0, 32)
        agather(B("OH", 0, 32), B("ZI"), B("offB", 16, 18))
        newlist(0, 32, "psP1")
        tt(B("TP"), B("IND"), B("PQ"), AL.mult)
        if last:
            tt(B("b1"), B("TP", 0, 16), B("TP", 16, 32), AL.add)
        site(32, V, "psD")
        if not last:
            for h in range(2):
                o = B("psP0", h, 16, 2)
                mm(o, B("I"), B(w, h, 16, 2), True, False)
                for f in range(3):
                    for e in range(2):
                        k = 128 * (2 * e + h)
                        mm(o, B("E", k, k + 128), B("TP", 16 * f + e, 16 * f + 16, 2), False, f == 2 and e == 1)
        if not last:
            site(0, 32, "psP1")
            putlist(32, V, "psD")
            vcopy(B(wn, 0, 16), B("psP0", 0, 16))
            putlist(0, 32, "psP1")
            send(t + 1, pieces(t + 1)[0])
            tt(B("b1"), B("TP", 0, 16), B("TP", 16, 32), AL.add)
        tt(B("bn"), B("TP", 32, 48), B("b1"), AL.add)
        ts(B("sc"), B("s2", 15, 256, 16), 6, None, AL.logical_shift_right)
        if last:
            site(0, 32, "psP1")
        tt(B(sown[1]), B("bn"), srcl, AL.add)
        if last:
            putlist(32, V, "psD")
        tt(B("d5"), B("sc"), B("F"), AL.subtract)
        ts(B("h1"), B(sown[1]), 13.0, None, AL.mult)
        if last:
            putlist(0, 32, "psP1")
        tt(B("d6"), B("d5"), acc, AL.mult)
        tt(B("h2"), B("h1"), B("sc"), AL.add)
        ts(B("h3"), B("h2"), 255, None, AL.bitwise_and)
        tt(B("d3"), B("h3"), n2, AL.subtract)
        if not last:
            tt(B("F"), B("d6"), B("F"), AL.add)
            tt(B("d4"), B("d3"), acc, AL.mult)
            tt(B(nown[1]), B("d4"), n2, AL.add)
            swap((nown[1], 0), 48)
            vcopy(B("acc%d" % t, 0, 16), acc)
            vcopy(B("acc%d" % t, 16, 32), acc)
            vcopy(B("n0U"), B("psS", 48, 64))
            k = 0
            for r in range(t + 1):
                for s in range(8):
                    mm(B("psS", 64, 80), B("BLK32"), B("acc%d" % r, 2 * s, 2 * s + 16), k == 0, k == 8 * (t + 1) - 1)
                    k += 1
            vcopy(B("Ai"), B("psS", 64, 80))
            ts(B("A7"), B("Ai"), 7, None, AL.bitwise_and)
            tt(B("thr"), B("F"), B("A7"), AL.subtract)
            ts(B("thr"), B("thr"), 64.0, None, AL.mult)
            nown, sown = nown[::-1], sown[::-1]
        else:
            tt(B("B2", 0, 256, 16), B("d6"), B("F"), AL.add)
            tt(B("d4"), B("d3"), acc, AL.mult)
            tt(B("B2", 1, 256, 16), B("d4"), n2, AL.add)
            vtrans(B("oT"), B("B2"))
            op("s", lambda e: e.dma_start(T.yf[:], T.oT[0:128:16, :]), [B("oT")], [], sem="st1", inc=16)
            op("a", lambda e: e.dma_start(T.yn[:], T.oT[1:128:16, :]), [B("oT")], [], sem="st2", inc=16)
    for s in sorted(total):
        if known["g"].get(s, 0) < total[s]:
            g.wait_ge(T.sem[s], total[s])
